import numpy as np, ml_dtypes
CORES = [6,15,38,47]
N = 4
BF = ml_dtypes.bfloat16
W, SV, M, HOPS = 4096, 1024, 256, [1, 1, 1, 1]
RO = len(HOPS) + 1
def names(rng, power, *shape):
    return np.minimum((W * rng.random(shape) ** power).astype(np.int64), W - 1)
def pairs(rng, C, power):
    a = names(rng, power, N, 8, 16, C); b = np.take_along_axis(a, np.argsort(rng.random((N, 8, 16, C)), axis=2), 2)
    share = rng.choice(np.array([0.0, 0.15, 0.5, 1.0]), (N, 8, 1, C)); b = np.where(rng.random(b.shape) < share, b, names(rng, power, N, 8, 16, C))
    fa = rng.choice(np.array([0.05, 0.12, 0.3, 0.7, 1.0]), (N, 8, 1, C), p=[0.2, 0.25, 0.2, 0.2, 0.15])
    fb = rng.choice(np.array([0.0, 0.3, 0.7, 1.0]), (N, 8, 1, C), p=[0.05, 0.25, 0.3, 0.4])
    return np.where(rng.random(a.shape) < fa, a, -1), np.where(rng.random(b.shape) < fb, b, -1)
def parts(rng, power):
    clk = rng.integers(0, 256, (N, 8, 16, W)); z = rng.integers(0, 256, (N, 8, 16, M)); th = rng.integers(1200, 1600, (N, 8))
    sc, st = pairs(rng, SV, power); d, t = pairs(rng, M, power)
    return clk, sc, st, d, t, z, th
def pack(clk, sc, st, d, t, z, th):
    return {"clk": clk.reshape(N, 128, W).astype(np.float32).astype(BF), "sc": sc.reshape(N, 128, SV).astype(np.int32), "st": st.reshape(N, 128, SV).astype(np.int32),
            "dl": d.reshape(N, 128, M).astype(np.int32), "tl": t.reshape(N, 128, M).astype(np.int32), "z0": z.reshape(N, 128, M).astype(np.float32).astype(BF),
            "th": np.repeat(th.reshape(N, 8), 16, axis=1).reshape(N, 128, 1).astype(np.int32)}
def setup_inputs(rng):
    return pack(*parts(rng, 1))
def setup_inputs_spread(rng):
    clk, sc, st, d, t, z, th = parts(rng, 4)
    clk = np.floor(np.exp2(8 * rng.random((N, 8, 1, W))) * rng.random((N, 8, 16, W))).astype(np.int64)
    z = np.floor(np.exp2(8 * rng.random((N, 8, 1, M))) * rng.random((N, 8, 16, M))).astype(np.int64)
    th = np.minimum(np.floor(np.exp2(12 * rng.random((N, 8)))).astype(np.int64), 4080)
    return pack(np.minimum(clk, 255), sc, st, d, t, np.minimum(z, 255), th)
def setup_inputs_ends(rng):
    def rec(C):
        p = rng.choice(np.array([0.0, 0.06, 0.5, 1.0]), (N, 8, 1, C)); s = (N, 8, 16, C)
        a = np.where(rng.random(s) < p, W - 1, -1)
        o = np.where(rng.random(s) < 0.3, -1, np.where(rng.random(s) < 0.15, W - 1, rng.integers(0, W, s)))
        return np.where(rng.random((N, 8, 1, C)) < 0.6, a, o)
    def half(C):
        k = rng.integers(0, 3, (N, 8, 1, C))
        return np.where(k == 0, 0, np.where(k == 1, 255, 255 * rng.integers(0, 2, (N, 8, 16, C))))
    clk = half(W); z = half(M); sc = rec(SV); st = rec(SV); d = rec(M); t = rec(M)
    g = np.arange(8)[None, :]; q = np.arange(N)[:, None]
    clk[..., 0] = 255; clk[..., W - 1] = np.where(((g + q + N) & 1) == 0, 255, 0)[:, :, None]
    clk[..., W - 2] = 255; clk[:, :, 15, W - 2] = 254
    z[..., 0] = 255; z[..., M - 1] = 255; z[..., M - 2] = 0
    th = 4080 * ((g // 2 + q + rng.integers(0, 2, (N, 1))) & 1); th[:, 5] = 4080
    for m, lo, hi in ((M - 1, 0, W - 1), (0, W - 1, 0)):
        d[..., m] = -1; d[:, :, 15, m] = W - 1; d[:, :, 4, m] = 5; t[..., m] = -1; t[:, :, 2, m] = lo; t[:, :, 15, m] = hi
    s = slice(M - 6, M - 2); z[..., s] = 255; d[:, :, 15, s] = W - 1; t[..., s] = -1; t[:, :, 2, s] = W - 2; t[:, :, 15, s] = 0
    d[:, 5] = W - 1; t[:, 5] = W - 1; sc[:, 5] = W - 1; st[:, 5] = W - 1; z[:, 5] = z[:, 5, :1]
    return pack(clk, sc, st, d, t, z, th)
def setup_inputs_corners(rng):
    clk, sc, st, d, t, z, th = parts(rng, 1)
    clk[:, 1::2, :, 1::2] = clk[:, 1::2, :, 0::2]
    th = rng.choice(np.array([0, 1, 126, 128, 1000, 1999, 4080]), (N, 8)); th[:, 0] = 1000; th[:, 7] = 1999; th[:, 3] = 0
    th[:, 5] = 2051 + 4 * rng.integers(0, 100, N); th[:, 6] = 2052 + 4 * rng.integers(0, 100, N)
    lanes = np.array([0, 1, SV - 1, SV, W - 2, W - 1])
    for q in range(N):
        for g in range(8):
            kind = rng.permutation(M) % 10; n = np.where(rng.random(M) < 0.5, rng.choice(lanes, M), rng.integers(0, W, M)); full = rng.integers(0, W, (16, M))
            D = d[q, g]; T = t[q, g]; x = clk[q, g][:, n]; room = np.maximum(x, 255 - x)
            gap = np.maximum(int(th[q, g]) + rng.integers(-1, 2, M), 0); step = np.clip(gap[None, :] - (np.add.accumulate(room, axis=0) - room), 0, room)
            near = np.where(x < 128, x + step, x - step)
            s = kind == 0; D[:, s] = -1; T[:, s] = -1; T[15, s] = n[s]
            s = kind == 1; D[:, s] = -1; T[:, s] = -1
            s = kind == 2; D[:, s] = full[:, s]; T[:, s] = -1
            s = kind == 3; D[:, s] = full[:, s]; T[:, s] = full[::-1][:, s]
            s = kind == 4; D[:, s] = n[s]; T[:, s] = -1; T[15, s] = n[s]
            s = kind == 5; D[:, s] = full[:, s] & ~1; T[:, s] = full[::-1][:, s] | 1
            s = kind == 6; D[:, s] = -1; D[15, s] = n[s]; T[:, s] = -1; T[0, s] = n[s]
            s = kind == 7; D[:, s] = -1; D[0, s] = n[s]; T[:, s] = -1; T[15, s] = n[s] ^ 1
            s = kind == 8; D[:, s] = -1; D[7, s] = n[s]; D[8, s] = (n[s] + 5) % W; T[:, s] = -1; T[15, s] = n[s]; T[3, s] = n[s] ^ 1
            s = kind == 9; D[:, s] = n[s]; D[0, s] = n[s] ^ 1; T[:, s] = n[s]
            s = (kind == 4) | (kind == 6) | (kind == 8) | (kind == 9); z[q, g][:, s] = near[:, s]
    k = rng.integers(0, 6, (N, 8, 1, SV)); more = rng.integers(0, W, (2, N, 8, 16, SV))
    st = np.where(k == 4, sc[:, :, ::-1], st)
    sc = np.where((k == 0) | (k == 2), -1, np.where(k == 1, more[0], sc)); st = np.where((k == 0) | (k == 3), -1, np.where(k == 1, more[1], st))
    return pack(clk, sc, st, d, t, z, th)
def setup_inputs_crowd(rng):
    clk, sc, st, d, t, z, th = parts(rng, 1); h = SV >> 1
    def high(*shape):
        return h + rng.integers(0, h - 1, shape) + SV * rng.integers(0, W // SV, shape)
    for q in range(N):
        for g in (0, 1):
            keep = d[q, g, :, M - 1].copy(), z[q, g, :, M - 1].copy()
            z[q, g] = rng.permuted(np.repeat(rng.integers(0, 256, (16, 1)), M, axis=1), axis=0); t[q, g] = -1
            if g == 1: d[q, g, :, M - 1], z[q, g, :, M - 1] = keep; t[q, g, 15, M - 1] = W - 1
        for g in (2, 3):
            v = int(rng.choice(np.array([0, SV - 1, SV >> 1]))); n = v + SV * rng.integers(0, W // SV, (16, M))
            t[q, g] = np.where(rng.random((16, M)) < 0.5, n, -1); t[q, g, 9] = n[9]; d[q, g] = -1
            if g == 3: d[q, g, 15, M - 1] = (v + 1) % W
        for g in (6, 7):
            n = rng.integers(0, W, M); z[q, g] = clk[q, g][:, n]; t[q, g, 5] = n
            d[q, g] = -1; d[q, g, 15] = n
            if g == 7: d[q, g, 15, M - 1] = -1
    for g, c, lim in ((4, 20, 219), (5, 35, 212)):
        clk[:, g] = rng.integers(0, 8, (N, 16, W)); clk[:, g, :, W - 1] = c
        d[:, g] = high(N, 16, M); t[:, g] = rng.permuted(d[:, g], axis=1)
        sc[:, g, :, :h] = high(N, 16, h); st[:, g, :, :h] = rng.permuted(sc[:, g, :, :h], axis=1)
        z[:, g] = rng.integers(0, 7, (N, 16, M))
        for q in range(N):
            z[q, g, :, M - 1] = 6 + (np.arange(16) < 4 + q)
            b = (q + int(np.sum(HOPS[:-1]))) % N; sc[b, g, :, 100 + q] = W - 1; st[b, g, :, 100 + q] = W - 1
            th[(b + HOPS[-1]) % N, g] = lim - q
    d[:, 5, 15, 0] = -1
    return pack(clk, sc, st, d, t, z, th)
def check_inputs(d):
    bad = []
    for k, lo, hi in (("clk", 0, 255), ("z0", 0, 255), ("sc", -1, W - 1), ("st", -1, W - 1), ("dl", -1, W - 1), ("tl", -1, W - 1), ("th", 0, 4080)):
        a = np.asarray(d[k]).astype(np.float64)
        if not (np.min(a) >= lo and np.max(a) <= hi): bad.append("range of " + k)
        elif np.any(a != np.floor(a)): bad.append("whole numbers in " + k)
    h = np.asarray(d["th"]).reshape(-1, 16)
    if np.any(h != h[:, :1]): bad.append("th alike in a group")
    return bad
def reference(clk, sc, st, dl, tl, z0, th):
    X = clk.astype(np.float32).astype(np.int64).reshape(N, 8, 16, W); Z = z0.astype(np.float32).astype(np.int64).reshape(N, 8, 16, M)
    C = sc.astype(np.int64).reshape(N, 8, 16, SV); S = st.astype(np.int64).reshape(N, 8, 16, SV)
    D = dl.astype(np.int64).reshape(N, 8, 16, M); T = tl.astype(np.int64).reshape(N, 8, 16, M)
    base = th.astype(np.int64).reshape(N, 8, 16)[:, :, 0]; A = np.zeros((N, 8), np.int64); row = np.arange(16).reshape(1, 16, 1)
    for visit in range(RO):
        nd, nt, nz = [], [], []
        for a in range(N):
            d, t, z = D[a], T[a], Z[a]
            x = np.take_along_axis(X[a], np.maximum(d, 0).reshape(8, 1, 16 * M), 2).reshape(8, 16, 16, M)
            y = np.take_along_axis(X[a], np.maximum(t, 0).reshape(8, 1, 16 * M), 2).reshape(8, 16, 16, M)
            dist = np.sum(np.abs(x - z[:, :, None, :]), axis=1)
            score = np.where(t >= 0, np.sum(np.minimum(y, z[:, :, None, :]), axis=1), -1)
            ks = np.argmax(score, axis=1)
            has = np.any(t >= 0, axis=1); v = np.take_along_axis(t, ks[:, None, :], 1)[:, 0] & (SV - 1)
            eq = (d[:, :, None, :] == t[:, None, :, :]) & (d >= 0)[:, :, None, :]
            cd = np.any(eq, axis=2); ct = np.any(eq, axis=1)
            lim = base[a] + 8 * (A[a] & 31)
            abort = np.any(cd & (dist > lim[:, None, None]), axis=1)
            d1 = np.where(cd, -1, d); t1 = np.where(ct | (row == ks[:, None, :]), -1, t)
            left = np.any(d1 >= 0, axis=1); proof = has & ~abort & ~left; go = has & ~abort & left
            yk = np.take_along_axis(y, ks[:, None, None, :], 2)[:, :, 0]
            top = np.max(np.where((d1 >= 0)[:, None, :, :], x, 0), axis=2)
            cv = np.take_along_axis(C[a], v[:, None, :], 2); sv = np.take_along_axis(S[a], v[:, None, :], 2)
            u = np.sum(z, axis=1) & (SV - 1)
            cu = np.take_along_axis(C[a], u[:, None, :], 2); su = np.take_along_axis(S[a], u[:, None, :], 2)
            hd = np.any(cv[:, :, None, :] == d[:, None, :, :], axis=2); ht = np.any(sv[:, :, None, :] == t[:, None, :, :], axis=2)
            d2 = np.where((d1 < 0) & ~hd, cv, d1); t2 = np.where((t1 < 0) & ~ht, sv, t1)
            ab = abort[:, None, :]; on = go[:, None, :]
            nd.append(np.where(ab, cv, np.where(on, d2, cu))); nt.append(np.where(ab, sv, np.where(on, t2, su)))
            nz.append(np.where(ab, np.abs(z - yk), np.where(on, (yk + top) >> 1, z)))
            A[a] += np.sum(cd & ~ab, axis=(1, 2))
            for g in range(8):
                for m in np.nonzero(proof[g])[0]: C[a, g, :, v[g, m]] = t1[g, :, m]
        D, T, Z = np.stack(nd), np.stack(nt), np.stack(nz)
        if visit < RO - 1: D, T, Z = [np.roll(b, HOPS[visit], axis=0) for b in (D, T, Z)]
    return {"yd": D.reshape(N, 128, M).astype(np.float32), "yt": T.reshape(N, 128, M).astype(np.float32), "yz": Z.reshape(N, 128, M).astype(np.float32), "ys": C.reshape(N, 128, SV).astype(np.float32)}

@@ -1,0 +1,501 @@
+from concourse.mybir import AluOpType, ActivationFunctionType
+
+A, F = AluOpType, ActivationFunctionType
+NV = 5
+f32, f16, b16, i32, u16 = "float32", "float16", "bfloat16", "int32", "uint16"
+SCRATCH, ALIAS = {}, {}
+
+
+def _decl(text, d, lead):
+    for w in text.split():
+        n, s = w.split(":")
+        SCRATCH[n] = ("sbuf", [128] + lead + [int(x) for x in s.split(",")], d)
+
+
+_decl("tli:256 dli:256 thi:1 sci:1024 sti:1024 pidx:1 pmi:1 ai:1 a31:1", i32, [])
+_decl("tm0:256 ts0:256 stm:1024 sta:1024 stw:1024 scw:1280 ysw:1280 pmf:1 iq:384 P1:16 on32:128 boa:128 bo32:128 id32:128 "
+      "q0i:16 q0:16 thn:1 nlim:8 asum:16 T1s:256 pr:16 dvq:16 mvq:16 PV:16 PVs:256 lm:16 dq2:16 lq:16 PLf:16 od:256 ot:256 oz:256 cst:4", f32, [])
+_decl("selm:2048 bc:2048 dM:384 tri:256 PV16:16 eqP:256", f16, [])
+_decl("clkw:4112 fsel:2048 rst:2048 rowc:128 k8big:128 k8m:8", b16, [])
+_decl("PLu:32", u16, [])
+_decl("eqA:2048 eqB:2048 eqC:2048 Dq:512 Tq:512 D1:128 KD:128 CD:128 T1a:128 CT:128 FC:128 oh:128 KT:128 T1:128 KTf:128 LMs:384 "
+      "cw:128 sw:128 hf:128", f16, [2])
+_decl("Y:2048 GA:16,128 XG:2048 xs:2048 rl:128 OHn:128 SG:128 SA:128 ac:128 acr:128 ysb:128 zg:128 yg:128", b16, [2])
+_decl("sk:128 sk2:128 a1:8 b1:8 sel:8 dvu:8 ms:8 wf:8 C1:128 C1t:128 Dm:128 Tm:128", f32, [2])
+_decl("nu:16 nv:16", i32, [2])
+_decl("D1u:128 nlu:8 wu:8", u16, [2])
+_decl("dt:128 tt:128 sd:128 stt:128", u16, [2 * NV])
+_decl("zl:128 sz:128", b16, [2 * NV])
+for _b, _l, _d in (("kh", "I16 Im16 BOm16 BO16 BOm128 c2048 o128h cm2047", f16),
+                   ("kb", "Ib Ibn Ibh Ib512n Ib256 Ib256n Ib4096n Ib65536 BO64b BOb c67584 cm4096 o128b", b16)):
+    _l = _l.split()
+    SCRATCH[_b] = ("sbuf", [128, len(_l), 128], _d)
+    for _i, _n in enumerate(_l):
+        ALIAS[_n] = (_b, _i)
+for _n in ("pc", "po", "pk", "r0", "r1", "r2"):
+    SCRATCH[_n] = ("psum", [128, 512], f32)
+SCRATCH["pg0"] = SCRATCH["pg1"] = ("psum", [128, 8, 64], f32)
+LOADS = ("tl", "dl", "za", "zb", "th", "clk", "st", "sc")
+SEMAPHORES = ["sv", "ss", "sp", "sg", "so", "ls"] + ["l_" + n for n in LOADS]
+SEMAPHORES += ["a%d%d%s" % (t, h, k) for t in range(1, NV) for h in (0, 1) for k in "dtz"]
+CYC, OVV, OVS, WAKE, SELF, REMOTE = 1.0, 55.0, 75.0, 70.0, 50.0, 2600.0
+
+
+def R(name, *ix):
+    return (ALIAS[name][0], (ALIAS[name][1],) + ix) if name in ALIAS else (name, ix)
+
+
+def S_(a, b, st=None):
+    return slice(a, b, st)
+
+
+def blk(i, n=128):
+    return slice(n * i, n * i + n)
+
+
+def get(T, x):
+    return T[x[0]][(slice(None),) + x[1] + (slice(None),) * (len(SCRATCH[x[0]][1]) - 1 - len(x[1]))]
+
+
+def span(x):
+    out = []
+    for d, n in enumerate(SCRATCH[x[0]][1][1:]):
+        i = x[1][d] if d < len(x[1]) else slice(None)
+        if isinstance(i, int):
+            out.append((i, i + 1, 1))
+        else:
+            a, b, st = i.indices(n)
+            out.append((a, b, len(range(a, b, st))))
+    return out
+
+
+def size(x):
+    n = 1
+    for s in span(x):
+        n *= s[2]
+    return n
+
+
+def psum(x):
+    return SCRATCH[x[0]][0] == "psum"
+
+
+def two(*xs):
+    return all(not psum(x) and SCRATCH[x[0]][2] in (f16, b16, u16) for x in xs)
+
+
+def program(nrem):
+    ops, rc = [], [0]
+
+    def add(e, dur, fn, r, w, **kw):
+        ops.append(dict(kw, e=e, d=dur, fn=fn, r=[x for x in r if isinstance(x, tuple)], w=w))
+        return len(ops) - 1
+
+    def val(T, x):
+        return get(T, x) if isinstance(x, tuple) else x
+
+    def ts(o, i, s1, op0, s2=None, op1=None):
+        def fn(g, T):
+            a = (get(T, o), get(T, i), val(T, s1), val(T, s2), op0)
+            return g.vector.tensor_scalar(*(a if op1 is None else a + (op1,)))
+        add("V", OVV + max(64, size(o) * (0.5 if two(o, i) else 1)) * CYC, fn, [i, s1, s2], [o])
+
+    def tt(o, a, b, op):
+        add("V", OVV + max(64, size(o) * (1 if psum(a) or psum(b) else 2)) * CYC,
+            lambda g, T: g.vector.tensor_tensor(get(T, o), get(T, a), get(T, b), op), [a, b], [o])
+
+    def cp(o, i):
+        add("V", OVV + max(64, size(o)) * CYC, lambda g, T: g.vector.tensor_copy(get(T, o), get(T, i)), [i], [o])
+
+    def fill(o, v):
+        add("V", OVV + max(64, size(o)) * CYC, lambda g, T: g.vector.memset(get(T, o), v), [], [o])
+
+    def scan(o, a, b):
+        add("V", OVV + size(o) * (0.5 if two(o, a, b) else 1) * CYC,
+            lambda g, T: g.vector.tensor_tensor_scan(get(T, o), get(T, a), get(T, b), 0.0, A.mult, A.max), [a, b], [o])
+
+    def act(o, i, func, bias=0.0, scale=1.0, acc=None):
+        def fn(g, T):
+            kw = {} if acc is None else {"accum_out": get(T, acc)}
+            return g.scalar.activation(get(T, o), get(T, i), func, bias=val(T, bias), scale=scale, **kw)
+        add("S", OVS + max(64, size(o)) * CYC, fn, [i, bias], [o] + ([] if acc is None else [acc]))
+
+    def gat(e, o, win, off):
+        def fn(g, T):
+            x = get(T, win).indirect(get(T, off))
+            return g.vector.tensor_copy(get(T, o), x) if e == "V" else g.scalar.activation(get(T, o), x, F.Copy)
+        add(e, OVS + 1.5 * size(o) * CYC, fn, [win, off], [o])
+
+    def mm(lst):
+        def fn(g, T):
+            x = None
+            for o, l, r, a, b in lst:
+                x = g.tensor.matmul(get(T, o), get(T, l), get(T, r), a, b)
+            return x
+        d = sum(6 + max(64, size(m[0])) * 0.5 * (4 if SCRATCH[m[1][0]][2] == f32 else 1) for m in lst)
+        add("P", 30 + d, fn, [m[1] for m in lst] + [m[2] for m in lst], [m[0] for m in lst])
+
+    def chain(o, *pairs):
+        return [(o, l, r, i == 0, i == len(pairs) - 1) for i, (l, r) in enumerate(pairs)]
+
+    def ring():
+        rc[0] += 1
+        return "r%d" % (rc[0] % 3)
+
+    def load(q, name, o, src, dur):
+        add(q, 60, lambda g, T: (g.sync if q == "Y" else g.scalar).dma_start(get(T, o), src(T)), [], [o], tok="l_" + name, lat=dur)
+    load("S", "clk", R("clkw", S_(16, 4112)), lambda T: T.clk[:, :], 5000)
+    load("Y", "tl", R("tli"), lambda T: T.tl[:, :], 2200)
+    load("Y", "dl", R("dli"), lambda T: T.dl[:, :], 2500)
+    load("Y", "za", R("zl", 0), lambda T: T.z0[:, 0:128], 2600)
+    load("Y", "zb", R("zl", 1), lambda T: T.z0[:, 128:256], 2700)
+    load("Y", "th", R("thi"), lambda T: T.th[:, :], 2800)
+    load("Y", "st", R("sti"), lambda T: T.st[:, :], 6500)
+    load("Y", "sc", R("sci"), lambda T: T.sc[:, :], 8000)
+
+    def iota(o, pat, base, cm=0):
+        kw = {} if SCRATCH[o[0]][2] == i32 else {"allow_small_or_imprecise_dtypes": True}
+        add("G", 130 + 2 * size(o), lambda g, T: g.iota(get(T, o), pat, base, cm, **kw), [], [o])
+
+    def aff(o, i, pat, op, base, cm):
+        add("G", 170 + 2 * size(o), lambda g, T: g.affine_select(get(T, o), get(T, i), pat, op, 0.0, base, cm), [i], [o])
+    fill(R("on32"), 1.0)
+    iota(R("pidx"), [[0, 1]], 0, 1)
+    aff(R("boa"), R("on32"), [[-16, 8], [0, 16]], A.is_ge, 0, 1)
+    aff(R("bo32"), R("boa"), [[16, 8], [0, 16]], A.is_ge, 15, -1)
+    aff(R("id32"), R("on32"), [[-1, 128]], A.is_equal, 0, 1)
+    iota(R("iq"), [[0, 24], [1, 16]], 0)
+    iota(R("rowc"), [[0, 8], [-1, 16]], 16)
+    iota(R("q0i"), [[16, 16]], 1024)
+    ts(R("pmi"), R("pidx"), 15, A.bitwise_and)
+    cp(R("pmf"), R("pmi"))
+    pm = R("pmf", S_(0, 1))
+    ts(R("P1"), R("iq", S_(0, 16)), pm, A.is_equal)
+    for j in range(16):
+        ts(R("bc", blk(j)), R("bo32"), R("P1", S_(j, j + 1)), A.mult)
+    ts(R("I16"), R("id32"), 1.0, A.mult)
+    ts(R("Im16"), R("id32"), -4112.0, A.mult)
+    fill(R("c2048"), 2048.0)
+    fill(R("clkw", S_(0, 16)), -1.0)
+    ts(R("BOm16"), R("bo32"), -4112.0, A.mult)
+    act(R("BOb"), R("bo32"), F.Copy)
+    for dst, src in (("selm", "BOm16"), ("fsel", "BOb")):
+        for j in range(16):
+            aff(R(dst, blk(j)), R(src), [[0, 8], [1, 16]], A.is_equal, -j, 0)
+    for n, src, k in (("Ib", "id32", 1), ("Ibn", "id32", -1), ("BO16", "bo32", 1), ("BOm128", "bo32", -128),
+                      ("BO64b", "bo32", 64), ("Ibh", "id32", 0.5), ("Ib512n", "id32", -512), ("Ib256", "id32", 256), ("k8big", "bo32", 8),
+                      ("Ib256n", "id32", -256), ("Ib4096n", "id32", -4096), ("Ib65536", "id32", 65536)):
+        if ALIAS.get(n, ("kb",))[0] == "kb":
+            act(R(n), R(src), F.Copy, scale=float(k))
+        else:
+            ts(R(n), R(src), float(k), A.mult)
+    ts(R("k8m"), R("bo32", S_(0, 128, 16)), -8.0, A.mult)
+    for n, x in (("o128b", 1.0 / 128), ("o128h", 1.0 / 128), ("cm2047", -2047.0), ("c67584", 67584.0), ("cm4096", -4096.0), ("rst", 1.0)):
+        fill(R(n), x)
+    fill(R("rst", S_(0, 2048, 16)), 0.0)
+    for i, x in enumerate((64.5, 0.5, -256.0, -1024.0)):
+        fill(R("cst", S_(i, i + 1)), x)
+    ts(R("dM"), R("iq"), pm, A.is_equal)
+    ts(R("tri"), R("iq", S_(0, 256)), pm, A.is_ge, 5000.0, A.mult)
+    ts(R("q0"), R("q0i"), pm, A.add)
+    ts(R("tm0"), R("tli"), 0.0, A.min, 2.0, A.mult)
+    tt(R("ts0"), R("tli"), R("tm0"), A.add)
+    for h in (0, 1):
+        ts(R("tt", h), R("ts0", blk(h)), 16.0, A.add)
+        ts(R("dt", h), R("dli", blk(h)), 16.0, A.add)
+    ts(R("thn"), R("thi"), -1.0, A.mult)
+    cp(R("nlim", S_(0, 1)), R("thn"))
+    for k in range(2):
+        c = blk(k, 512)
+        ts(R("stm", c), R("sti", c), 0.0, A.min, 2.0, A.mult)
+        tt(R("sta", c), R("sti", c), R("stm", c), A.add)
+        act(R("stw", c), R("sta", c), F.Copy, bias=-2047.0)
+    ts(R("scw", S_(0, 1024)), R("sci"), -2047.0, A.add)
+
+    WIN = R("clkw")
+    sent = {}
+
+    def arrive(t, h, kind, buf):
+        if t:
+            add("R", 0, None, [], [R(buf, 2 * t + h)], tok="a%d%d%s" % (t, h, kind), inc=nrem, after=sent[(t - 1, h, kind)])
+
+    def send(t, h, kind, src, buf):
+        def fn(g, T):
+            return get(T, R(buf, 2 * t + h + 2)), get(T, R(src, 2 * t + h)), "a%d%d%s" % (t + 1, h, kind)
+        sent[(t, h, kind)] = add("G", 100, fn, [R(src, 2 * t + h)], [], n="send")
+
+    def member(rows, held, eq, h):
+        for q in range(4):
+            b = ring()
+            mm([(R(b, blk(i)), R("bc", blk(4 * q + i)), R(rows, h, S_(0, 128)), True, True) for i in range(4)])
+            tt(R(eq, h, blk(q, 512)), R(held, h, S_(0, 512)), R(b, S_(0, 512)), A.is_equal)
+
+    def counts(eq, h):
+        return [(R("selm", blk(j)), R(eq, h, blk(j))) for j in range(16)]
+
+    def stageA(t, h):
+        k = 2 * t + h
+        arrive(t, h, "t", "tt")
+        arrive(t, h, "d", "dt")
+        arrive(t, h, "z", "zl")
+        for hb in (0, 1):
+            gat("S", R("Y", h, blk(hb, 1024)), WIN, R("tt", k, blk(hb, 64)))
+        for dst, src in (("Tq", "tt"), ("Dq", "dt")):
+            for r in range(4):
+                ts(R(dst, h, blk(r)), R(src, k), -2063.0, A.add)
+        D, Tn = R("Dq", h, S_(0, 128)), R("Tq", h, S_(0, 128))
+        member("Tq", "Dq", "eqA", h)
+        pD, pT, c = R("pc", S_(0, 128)), R("pc", S_(128, 256)), (R("I16"), R("c2048"))
+        mm(chain(pD, c, *[(R("Im16"), R("eqA", h, blk(j))) for j in range(16)]))
+        mm(chain(pT, c, *counts("eqA", h)))
+        tt(R("D1", h), D, pD, A.min)
+        tt(R("T1a", h), Tn, pT, A.min)
+        ts(R("D1u", h), R("D1", h), -2048.0, A.max, 2063.0, A.add)
+        ts(R("CT", h), R("T1a", h), -2055.0, A.is_lt)
+        ts(R("KD", h), R("D1", h), -2047.5, A.is_gt)
+        ts(R("CD", h), R("D1", h), -2055.0, A.is_lt)
+        for hb in (0, 1):
+            for q in (0, 1):
+                b = "pg%d" % q
+                mm(sum([chain(R(b, i), (R("Ib"), R("Y", h, S_(1024 * hb + 8 * q + i, 1024 * hb + 1024, 16))), (R("Ibn"), R("zl", k, blk(hb, 64))))
+                        for i in range(8)], []))
+                act(R("GA", h, blk(q, 8), blk(hb, 64)), R(b), F.Abs)
+        b = ring()
+        mm(chain(R(b, S_(0, 128)), *[(R("fsel", blk(j)), R("GA", h, j)) for j in range(16)]))
+        act(R("rl", h), R(b, S_(0, 128)), F.Relu, bias=R("nlim", S_(t, t + 1)))
+
+    def stageB(t, h):
+        k = 2 * t + h
+        Z, D, Tn = R("zl", k), R("Dq", h, S_(0, 128)), R("Tq", h, S_(0, 128))
+        kk, rs = R("pk", S_(0, 128)), R("rst", S_(0, 128))
+        kj = [R("pk", S_(j, 128, 16)) for j in range(16)]
+        mm([(kk, Z, R("k8big"), True, False), (kk, R("o128b"), R("rowc"), False, False)] +
+           [(kj[j], R("Y", h, S_(j, 2048, 16)), R("k8big", S_(0, 128, 16)), False, False) for j in range(16)] +
+           [(kj[j], R("GA", h, j), R("k8m"), False, j == 15) for j in range(16)])
+        scan(R("sk", h), rs, kk)
+        cp(R("sk", h, S_(0, 128, 16)), R("sk", h, S_(15, 128, 16)))
+        scan(R("sk2", h), rs, R("sk", h))
+        tt(R("oh", h), R("sk2", h), kk, A.is_equal)
+        o1, o2 = R("po", S_(0, 128)), R("po", S_(128, 256))
+        mm(chain(o1, (R("oh", h), R("I16"))) + chain(o2, (R("oh", h), R("Im16")), (R("I16"), R("c2048"))))
+        tt(R("KT", h), Tn, o1, A.mult)
+        act(R("OHn", h), o1, F.Copy)
+        tt(R("FC", h), R("rl", h), R("CT", h), A.min)
+        tt(R("T1", h), R("T1a", h), o2, A.min)
+        b = ring()
+        c = [R(b, blk(i)) for i in range(4)]
+        KD, FC, OHn, KT, BO = R("KD", h), R("FC", h), R("OHn", h), R("KT", h), R("BO16")
+        mm(chain(c[2], (R("o128h"), R("cm2047")), (Z, R("BOb"))) + chain(c[1], (KT, BO)) +
+           chain(c[0], (KD, BO), (FC, R("BOm128")), (OHn, R("BO64b"))) + chain(c[3], (BO, KD), (R("BOm128"), FC), (R("BO64b"), OHn)))
+        tt(R("LMs", h), R("dM"), R(b, S_(0, 384)), A.mult)
+        tt(R("ac", h), R("CD", h), c[3], A.min)
+        act(R("SG", h), c[3], F.Sign, bias=R("cst", S_(0, 1)), scale=-1.0)
+        act(R("SA", h), c[3], F.Sign, bias=R("cst", S_(1, 2)))
+        b = ring()
+        mm([(R(b, blk(i, 8)), R("LMs", h, blk(i)), R("BO16", S_(0, 128, 16)), True, True) for i in range(3)])
+        X, E = R(b, S_(0, 8)), R(b, S_(8, 16))
+        ts(R("nu", h), R(b, S_(8, 24)), 2047.0, A.add)
+        ts(R("a1", h), X, 64.5, A.is_gt)
+        ts(R("b1", h), X, -0.5, A.is_lt)
+        ts(R("nv", h), R("nu", h), 1023, A.bitwise_and)
+        ts(R("nlu", h), E, 2063.0, A.add)
+        tt(R("sel", h), R("a1", h), R("b1", h), A.add)
+        v, u = R("nv", h, S_(0, 8)), R("nv", h, S_(8, 16))
+        tt(R("dvu", h), v, u, A.subtract)
+        ts(R("pr", blk(h, 8)), X, 64.0, A.is_equal)
+        tt(R("ms", h), R("dvu", h), R("sel", h), A.mult)
+        tt(R("wf", h), R("ms", h), u, A.add)
+        cp(R("wu", h), R("wf", h))
+        gat("V", R("sw", h), R("stw"), R("wu", h))
+        gat("V", R("cw", h), R("scw", S_(0, 1024)), R("wu", h))
+        gat("S", R("ysb", h), WIN, R("nlu", h))
+        act(R("acr", h), R("ac", h), F.Relu, acc=R("asum", S_(k, k + 1)))
+        if t + 1 < NV and h == 1:
+            b = ring()
+            mm(chain(R(b, S_(0, 1)), *[(R("bo32"), R("asum", S_(i, i + 1))) for i in range(2 * t + 2)]))
+            cp(R("ai"), R(b, S_(0, 1)))
+            ts(R("a31"), R("ai"), 31, A.bitwise_and)
+            ts(R("nlim", S_(t + 1, t + 2)), R("a31"), -8.0, A.mult, R("thn"), A.add)
+        ts(R("KTf", h), R("T1", h), -2047.5, A.is_gt)
+        last = t == NV - 1
+        ts(R("T1s", blk(h)), R("T1", h), 2047.0 if last else 0.0, A.add, -1.0 if last else -2048.0, A.max)
+        for hb in (0, 1):
+            gat("S", R("XG", h, blk(hb, 1024)), WIN, R("D1u", h, blk(hb, 64)))
+
+    def out(name, buf, c):
+        add("Y", 60, lambda g, T: g.sync.dma_start(T[name][:, c], get(T, R(buf, c))), [R(buf, c)], [], tok="so")
+
+    def stageC(t, h):
+        k, last = 2 * t + h, t == NV - 1
+        SG, Ib = R("SG", h), R("Ib")
+        for x, held, cw, eq, c1, m, keep, one, snd, land, low in (("t", "Tq", "sw", "eqC", "C1t", "Tm", "KTf", "T1", "stt", "tt", -2050.0),
+                                                                  ("d", "Dq", "cw", "eqB", "C1", "Dm", "KD", "D1", "sd", "dt", -2048.0)):
+            member(cw, held, eq, h)
+            b = ring()
+            p0, p1 = R(b, S_(0, 128)), R(b, S_(128, 256))
+            mm(chain(p1, (R("I16"), R(one, h)), (R("Ib4096n"), SG), (Ib, R("cm4096"))) +
+               chain(p0, (Ib, R("c67584")), (R("Ib65536"), SG), (R("Im16"), R(keep, h)), *counts(eq, h)))
+            tt(R(c1, h), R(cw, h), p0, A.min)
+            tt(R(m, h), R(c1, h), p1, A.max)
+            if last:
+                ts(R("o" + x, blk(h)), R(m, h), 2047.0, A.add, -1.0, A.max)
+                out("y" + x, "o" + x, blk(h))
+            else:
+                ts(R(snd, k), R(m, h), low, A.max, 2063.0, A.add)
+                send(t, h, x, snd, land)
+        scan(R("xs", h), R("rst"), R("XG", h))
+        b = ring()
+        c = [R(b, blk(i)) for i in range(3)]
+        ys = R("ysb", h)
+        mm(chain(c[0], (R("Ibh"), ys), (R("Ibh"), R("xs", h, S_(15, 2048, 16))), (R("Ib512n"), SG)) +
+           chain(c[1], (Ib, R("zl", k)), (R("Ib256"), SG)) + chain(c[2], (Ib, ys), (R("Ib256n"), R("SA", h))))
+        ts(R("hf", h), c[0], 511.75, A.add, 1024.0, A.max)
+        act(R("zg", h), c[1], F.Relu, bias=R("cst", S_(2, 3)))
+        act(R("yg", h), c[2], F.Relu, bias=R("cst", S_(2, 3)))
+        p = R(ring(), S_(0, 128))
+        mm(chain(p, (R("I16"), R("hf", h)), (Ib, R("zg", h)), (R("Ibn"), R("yg", h))))
+        act(R("oz", blk(h)) if last else R("sz", k), p, F.Abs, bias=R("cst", S_(3, 4)))
+        if last:
+            out("yz", "oz", blk(h))
+        else:
+            send(t, h, "z", "sz", "zl")
+
+    def stageD(t):
+        last = t == NV - 1
+        for h in (0, 1):
+            tt(R("dvq", blk(h, 8)), R("nv", h, S_(0, 8)), R("q0", blk(h, 8)), A.subtract)
+        tt(R("mvq"), R("dvq"), R("pr"), A.mult)
+        tt(R("PV16"), R("mvq"), R("q0"), A.add)
+        tt(R("PV"), R("mvq"), R("q0"), A.add)
+        b = ring()
+        mm([(R(b, S_(r, 256, 16)), R("I16"), R("PV16"), True, True) for r in range(16)])
+        act(R("PVs"), R(b, S_(0, 256)), F.Copy)
+        b = ring()
+        mm([(R(b, S_(0, 256)), R("I16"), R("tri"), True, False)] +
+           [(R(b, S_(r, 256, 16)), R("bc", blk(r)), R("PV16"), False, r == 15) for r in range(16)])
+        tt(R("eqP"), R("PVs"), R(b, S_(0, 256)), A.is_equal)
+        b = ring()
+        mm(chain(R(b, S_(0, 16)), *[(R("selm", blk(r)), R("eqP", S_(r, 256, 16))) for r in range(16)]))
+        tt(R("dq2"), R("q0"), R("PV"), A.subtract)
+        ts(R("lm"), R(b, S_(0, 16)), -1.0, A.is_lt)
+        tt(R("lq"), R("lm"), R("dq2"), A.mult)
+        tt(R("PLf"), R("lq"), R("PV"), A.add)
+        cp(R("PLu", S_(0, 32, 2)), R("PLf"))
+        win = "ysw" if last else "scw"
+        if last:
+            ts(R("ysw", S_(0, 1024)), R("scw", S_(0, 1024)), 2047.0, A.add, -1.0, A.max)
+        for c in range(16):
+            o, off, src = R(win), R("PLu", S_(2 * c, 2 * c + 1)), R("T1s", blk(c, 16))
+            add("V", OVV + 64, lambda g, T, o=o, off=off, src=src: g.vector.tensor_copy(get(T, o).indirect(get(T, off)), get(T, src)), [off, src], [o])
+        if last:
+            out("ys", "ysw", S_(0, 1024))
+
+    for t in range(NV):
+        for stage in (stageA, stageB, stageC):
+            stage(t, 0)
+            stage(t, 1)
+        stageD(t)
+    return ops
+
+
+def depend(ops):
+    hist = {}
+    for i, o in enumerate(ops):
+        pw, acc = set(), {}
+        for x, wr in [(x, False) for x in o["r"]] + [(x, True) for x in o["w"]]:
+            sp = () if psum(x) else tuple(s[:2] for s in span(x))
+            acc[(x[0], sp)] = acc.get((x[0], sp), False) or wr
+        for (name, sp), wr in acc.items():
+            for j, sj, wj in hist.get(name, ()):
+                if j != i and all(a[0] < b[1] and b[0] < a[1] for a, b in zip(sp, sj)):
+                    if wj or wr or ops[j]["e"] != o["e"] and SCRATCH[name][0] == "psum":
+                        pw.add(j)
+        for (name, sp), wr in acc.items():
+            h = hist.setdefault(name, [])
+            if wr:
+                h[:] = [y for y in h if y[0] == i or not all(a[0] <= b[0] and b[1] <= a[1] for a, b in zip(sp, y[1]))]
+            h.append((i, sp, wr))
+        o["pw"] = pw
+
+
+def schedule(ops):
+    n = len(ops)
+    succ, cnt = [[] for _ in range(n)], [0] * n
+    for i, o in enumerate(ops):
+        ps = [(j, WAKE if ops[j]["e"] != o["e"] else SELF) for j in o["pw"]]
+        if "after" in o:
+            ps.append((o["after"], REMOTE))
+        cnt[i] = len(ps)
+        for j, l in ps:
+            succ[j].append((i, l))
+    fin = [o["d"] + o.get("lat", 0.0) for o in ops]
+    pri = [0.0] * n
+    for i in range(n - 1, -1, -1):
+        pri[i] = fin[i] + max([0.0] + [l + pri[k] for k, l in succ[i]])
+    rdy, free, order = [0.0] * n, {}, []
+    ready = [i for i in range(n) if cnt[i] == 0]
+    while ready:
+        st = {i: max(rdy[i], free.get(ops[i]["e"], 0.0)) for i in ready}
+        tmin = min(st.values()) + 1.0
+        i = max((j for j in ready if st[j] <= tmin), key=lambda j: pri[j])
+        ready.remove(i)
+        o, s = ops[i], st[i]
+        o["s"] = s
+        if o["e"] != "R":
+            free[o["e"]] = s + o["d"]
+        order.append(i)
+        for k, l in succ[i]:
+            cnt[k] -= 1
+            rdy[k] = max(rdy[k], s + fin[i] + l)
+            if cnt[k] == 0:
+                ready.append(k)
+    return order
+
+
+CACHE = {}
+
+
+def rank_program(g, core, T, topo):
+    rank = T.rank_of(core)
+    if rank is None:
+        return
+    dst = T.cores[(rank + 1) % len(T.cores)]
+    rid, pid = topo.addr(dst)[:2]
+    mask, nrem = topo.mask(core, dst), len(topo.engines(core, dst))
+    if nrem not in CACHE:
+        ops = program(nrem)
+        depend(ops)
+        CACHE[nrem] = (ops, schedule(ops))
+    ops, order = CACHE[nrem]
+    queue = {"V": g.vector, "S": g.scalar, "P": g.tensor, "G": g, "Y": g.sync}
+    sem = {"V": "sv", "S": "ss", "P": "sp", "G": "sg"}
+    known, vc, tok, total = {e: {} for e in queue}, {}, {}, {"ls": 0}
+    for i in order:
+        o = ops[i]
+        e = o["e"]
+        if e == "R":
+            tok[i], vc[i] = (o["tok"], o["inc"]), {}
+            total[o["tok"]] = o["inc"]
+            continue
+        kn, need = known[e], {}
+        for j in o["pw"]:
+            need[tok[j][0]] = max(need.get(tok[j][0], 0), tok[j][1])
+        for j in sorted(o["pw"], reverse=True):
+            s = tok[j][0]
+            if kn.get(s, 0) < need[s]:
+                queue[e].wait_ge(T.sem[s], need[s])
+                kn[s] = need[s]
+            for a in vc[j]:
+                kn[a] = max(kn.get(a, 0), vc[j][a])
+        x = o["fn"](g, T)
+        if o.get("n") == "send":
+            g.remote_dma(out_ap=x[0], in_ap=x[1], remote_sem=T.sem[x[2]], local_sem=T.sem["ls"], pid=pid, routing_id=rid, dma_engine_mask=mask)
+            total["ls"] += nrem
+            continue
+        s, n = (o["tok"], 16) if "tok" in o else (sem[e], 1)
+        total[s] = total.get(s, 0) + n
+        x.then_inc(T.sem[s], n)
+        tok[i], vc[i] = (s, total[s]), dict(kn)
+    for s in total:
+        if total[s]:
+            g.wait_ge(T.sem[s], total[s])

@@ -16,18 +16,18 @@ _decl("tli:256 dli:256 thi:1 sci:1024 sti:1024 pidx:1 pmi:1 ai:1 a31:1", i32, []
 _decl("tm0:256 ts0:256 stm:1024 sta:1024 stw:1024 scw:1280 ysw:1280 pmf:1 iq:384 P1:16 on32:128 boa:128 bo32:128 id32:128 "
       "q0i:16 q0:16 thn:1 nlim:8 asum:16 T1s:256 pr:16 dvq:16 mvq:16 PV:16 PVs:256 lm:16 dq2:16 lq:16 PLf:16 od:256 ot:256 oz:256 cst:4", f32, [])
 _decl("selm:2048 bc:2048 dM:384 tri:256 PV16:16 eqP:256", f16, [])
-_decl("clkw:4112 fsel:2048 rst:2048 rowc:128 k8big:128 k8m:8", b16, [])
+_decl("clkw:4112 rst:2048 rowc:128 k8big:128", b16, [])
 _decl("PLu:32", u16, [])
 _decl("eqA:2048 eqB:2048 eqC:2048 Dq:512 Tq:512 D1:128 KD:128 CD:128 T1a:128 CT:128 FC:128 oh:128 KT:128 T1:128 KTf:128 LMs:384 "
-      "cw:128 sw:128 hf:128", f16, [2])
-_decl("Y:2048 GA:16,128 XG:2048 xs:2048 rl:128 OHn:128 SG:128 SA:128 ac:128 acr:128 ysb:128 zg:128 yg:128", b16, [2])
+      "cw:128 sw:128 hf:128 dst:128", f16, [2])
+_decl("Y:2048 GA:16,128 XG:2048 xs:2048 rl:128 OHn:128 SG:128 SA:128 ac:128 acr:128 cmA:128 cmB:128 cmC:128 ysb:128 zg:128 yg:128", b16, [2])
 _decl("sk:128 sk2:128 a1:8 b1:8 sel:8 dvu:8 ms:8 wf:8 C1:128 C1t:128 Dm:128 Tm:128", f32, [2])
 _decl("nu:16 nv:16", i32, [2])
 _decl("D1u:128 nlu:8 wu:8", u16, [2])
 _decl("dt:128 tt:128 sd:128 stt:128", u16, [2 * NV])
 _decl("zl:128 sz:128", b16, [2 * NV])
-for _b, _l, _d in (("kh", "I16 Im16 BOm16 BO16 BOm128 c2048 o128h cm2047", f16),
-                   ("kb", "Ib Ibn Ibh Ib512n Ib256 Ib256n Ib4096n Ib65536 BO64b BOb c67584 cm4096 o128b", b16)):
+for _b, _l, _d in (("kh", "I16 Im16 BOm16 BO16 BOm128 c2048 c2040 c16320n I8n o128h cm2047", f16),
+                   ("kb", "Ib Ibn Ibh Ib512n Ib256 Ib256n Ib4096n Ib65536 I4128n BO64b BOb c67584 cm4096 o128b", b16)):
     _l = _l.split()
     SCRATCH[_b] = ("sbuf", [128, len(_l), 128], _d)
     for _i, _n in enumerate(_l):
@@ -38,7 +38,7 @@ SCRATCH["pg0"] = SCRATCH["pg1"] = ("psum", [128, 8, 64], f32)
 LOADS = ("tl", "dl", "za", "zb", "th", "clk", "st", "sc")
 SEMAPHORES = ["sv", "ss", "sp", "sg", "so", "ls"] + ["l_" + n for n in LOADS]
 SEMAPHORES += ["a%d%d%s" % (t, h, k) for t in range(1, NV) for h in (0, 1) for k in "dtz"]
-CYC, OVV, OVS, WAKE, SELF, REMOTE = 1.0, 55.0, 75.0, 70.0, 50.0, 2600.0
+CYC, OVV, OVS, WAKE, SELF, REMOTE = 0.9, 10.0, 20.0, 70.0, 50.0, 3000.0
 
 
 def R(name, *ix):
@@ -124,7 +124,7 @@ def program(nrem):
         def fn(g, T):
             x = get(T, win).indirect(get(T, off))
             return g.vector.tensor_copy(get(T, o), x) if e == "V" else g.scalar.activation(get(T, o), x, F.Copy)
-        add(e, OVS + 1.5 * size(o) * CYC, fn, [win, off], [o])
+        add(e, 75 + 1.5 * size(o) * CYC, fn, [win, off], [o])
 
     def mm(lst):
         def fn(g, T):
@@ -137,10 +137,6 @@ def program(nrem):
 
     def chain(o, *pairs):
         return [(o, l, r, i == 0, i == len(pairs) - 1) for i, (l, r) in enumerate(pairs)]
-
-    def ring():
-        rc[0] += 1
-        return "r%d" % (rc[0] % 3)
 
     def load(q, name, o, src, dur):
         add(q, 60, lambda g, T: (g.sync if q == "Y" else g.scalar).dma_start(get(T, o), src(T)), [], [o], tok="l_" + name, lat=dur)
@@ -173,24 +169,19 @@ def program(nrem):
     ts(R("P1"), R("iq", S_(0, 16)), pm, A.is_equal)
     for j in range(16):
         ts(R("bc", blk(j)), R("bo32"), R("P1", S_(j, j + 1)), A.mult)
-    ts(R("I16"), R("id32"), 1.0, A.mult)
-    ts(R("Im16"), R("id32"), -4112.0, A.mult)
-    fill(R("c2048"), 2048.0)
     fill(R("clkw", S_(0, 16)), -1.0)
-    ts(R("BOm16"), R("bo32"), -4112.0, A.mult)
-    act(R("BOb"), R("bo32"), F.Copy)
-    for dst, src in (("selm", "BOm16"), ("fsel", "BOb")):
-        for j in range(16):
-            aff(R(dst, blk(j)), R(src), [[0, 8], [1, 16]], A.is_equal, -j, 0)
-    for n, src, k in (("Ib", "id32", 1), ("Ibn", "id32", -1), ("BO16", "bo32", 1), ("BOm128", "bo32", -128),
-                      ("BO64b", "bo32", 64), ("Ibh", "id32", 0.5), ("Ib512n", "id32", -512), ("Ib256", "id32", 256), ("k8big", "bo32", 8),
+    for n, src, k in (("I16", "id32", 1), ("Im16", "id32", -4112), ("BO16", "bo32", 1), ("BOm16", "bo32", -4112), ("BOm128", "bo32", -128),
+                      ("Ib", "id32", 1), ("Ibn", "id32", -1), ("I4128n", "id32", -4128), ("BOb", "bo32", 1), ("BO64b", "bo32", 64),
+                      ("Ibh", "id32", 0.5), ("Ib512n", "id32", -512), ("Ib256", "id32", 256), ("I8n", "id32", -8), ("k8big", "bo32", 8),
                       ("Ib256n", "id32", -256), ("Ib4096n", "id32", -4096), ("Ib65536", "id32", 65536)):
         if ALIAS.get(n, ("kb",))[0] == "kb":
             act(R(n), R(src), F.Copy, scale=float(k))
         else:
             ts(R(n), R(src), float(k), A.mult)
-    ts(R("k8m"), R("bo32", S_(0, 128, 16)), -8.0, A.mult)
-    for n, x in (("o128b", 1.0 / 128), ("o128h", 1.0 / 128), ("cm2047", -2047.0), ("c67584", 67584.0), ("cm4096", -4096.0), ("rst", 1.0)):
+    for j in range(16):
+        aff(R("selm", blk(j)), R("BOm16"), [[0, 8], [1, 16]], A.is_equal, -j, 0)
+    for n, x in (("c2048", 2048.0), ("o128b", 1.0 / 128), ("o128h", 1.0 / 128), ("cm2047", -2047.0), ("c2040", 2040.0), ("c16320n", -16320.0),
+                 ("c67584", 67584.0), ("cm4096", -4096.0), ("rst", 1.0)):
         fill(R(n), x)
     fill(R("rst", S_(0, 2048, 16)), 0.0)
     for i, x in enumerate((64.5, 0.5, -256.0, -1024.0)):
@@ -226,12 +217,15 @@ def program(nrem):
 
     def member(rows, held, eq, h):
         for q in range(4):
-            b = ring()
+            rc[0] += 1
+            b = "r%d" % (rc[0] % 2)
             mm([(R(b, blk(i)), R("bc", blk(4 * q + i)), R(rows, h, S_(0, 128)), True, True) for i in range(4)])
             tt(R(eq, h, blk(q, 512)), R(held, h, S_(0, 512)), R(b, S_(0, 512)), A.is_equal)
 
-    def counts(eq, h):
-        return [(R("selm", blk(j)), R(eq, h, blk(j))) for j in range(16)]
+    def counts(eq, cm, h, b):
+        mm([(R(b, S_(384 + j, 512, 16)), R(eq, h, blk(j)), R("BO16", S_(0, 128, 16)), True, True) for j in range(16)])
+        act(R(cm, h), R(b, S_(384, 512)), F.Copy)
+        return (R(cm, h), R("I4128n"))
 
     def stageA(t, h):
         k = 2 * t + h
@@ -247,7 +241,7 @@ def program(nrem):
         member("Tq", "Dq", "eqA", h)
         pD, pT, c = R("pc", S_(0, 128)), R("pc", S_(128, 256)), (R("I16"), R("c2048"))
         mm(chain(pD, c, *[(R("Im16"), R("eqA", h, blk(j))) for j in range(16)]))
-        mm(chain(pT, c, *counts("eqA", h)))
+        mm(chain(pT, c, counts("eqA", "cmA", h, "po")))
         tt(R("D1", h), D, pD, A.min)
         tt(R("T1a", h), Tn, pT, A.min)
         ts(R("D1u", h), R("D1", h), -2048.0, A.max, 2063.0, A.add)
@@ -260,18 +254,19 @@ def program(nrem):
                 mm(sum([chain(R(b, i), (R("Ib"), R("Y", h, S_(1024 * hb + 8 * q + i, 1024 * hb + 1024, 16))), (R("Ibn"), R("zl", k, blk(hb, 64))))
                         for i in range(8)], []))
                 act(R("GA", h, blk(q, 8), blk(hb, 64)), R(b), F.Abs)
-        b = ring()
-        mm(chain(R(b, S_(0, 128)), *[(R("fsel", blk(j)), R("GA", h, j)) for j in range(16)]))
-        act(R("rl", h), R(b, S_(0, 128)), F.Relu, bias=R("nlim", S_(t, t + 1)))
+        d = R("pc", S_(256, 384))
+        mm([(R("pc", S_(256 + j, 384, 16)), R("GA", h, j), R("BOb", S_(0, 128, 16)), True, True) for j in range(16)])
+        ts(R("dst", h), d, -2040.0, A.add)
+        mm(chain(d, (R("dst", h), R("I16")), (R("I16"), R("c2040"))))
+        act(R("rl", h), d, F.Relu, bias=R("nlim", S_(t, t + 1)))
 
     def stageB(t, h):
         k = 2 * t + h
-        Z, D, Tn = R("zl", k), R("Dq", h, S_(0, 128)), R("Tq", h, S_(0, 128))
+        Z, Tn = R("zl", k), R("Tq", h, S_(0, 128))
         kk, rs = R("pk", S_(0, 128)), R("rst", S_(0, 128))
-        kj = [R("pk", S_(j, 128, 16)) for j in range(16)]
-        mm([(kk, Z, R("k8big"), True, False), (kk, R("o128b"), R("rowc"), False, False)] +
-           [(kj[j], R("Y", h, S_(j, 2048, 16)), R("k8big", S_(0, 128, 16)), False, False) for j in range(16)] +
-           [(kj[j], R("GA", h, j), R("k8m"), False, j == 15) for j in range(16)])
+        mm([(kk, Z, R("k8big"), True, False), (kk, R("o128b"), R("rowc"), False, False), (kk, R("o128h"), R("c16320n"), False, False)] +
+           [(R("pk", S_(j, 128, 16)), R("Y", h, S_(j, 2048, 16)), R("k8big", S_(0, 128, 16)), False, False) for j in range(16)] +
+           [(kk, R("I8n"), R("dst", h), False, True)])
         scan(R("sk", h), rs, kk)
         cp(R("sk", h, S_(0, 128, 16)), R("sk", h, S_(15, 128, 16)))
         scan(R("sk2", h), rs, R("sk", h))
@@ -282,7 +277,7 @@ def program(nrem):
         act(R("OHn", h), o1, F.Copy)
         tt(R("FC", h), R("rl", h), R("CT", h), A.min)
         tt(R("T1", h), R("T1a", h), o2, A.min)
-        b = ring()
+        b = "r2"
         c = [R(b, blk(i)) for i in range(4)]
         KD, FC, OHn, KT, BO = R("KD", h), R("FC", h), R("OHn", h), R("KT", h), R("BO16")
         mm(chain(c[2], (R("o128h"), R("cm2047")), (Z, R("BOb"))) + chain(c[1], (KT, BO)) +
@@ -291,7 +286,6 @@ def program(nrem):
         tt(R("ac", h), R("CD", h), c[3], A.min)
         act(R("SG", h), c[3], F.Sign, bias=R("cst", S_(0, 1)), scale=-1.0)
         act(R("SA", h), c[3], F.Sign, bias=R("cst", S_(1, 2)))
-        b = ring()
         mm([(R(b, blk(i, 8)), R("LMs", h, blk(i)), R("BO16", S_(0, 128, 16)), True, True) for i in range(3)])
         X, E = R(b, S_(0, 8)), R(b, S_(8, 16))
         ts(R("nu", h), R(b, S_(8, 24)), 2047.0, A.add)
@@ -311,9 +305,9 @@ def program(nrem):
         gat("S", R("ysb", h), WIN, R("nlu", h))
         act(R("acr", h), R("ac", h), F.Relu, acc=R("asum", S_(k, k + 1)))
         if t + 1 < NV and h == 1:
-            b = ring()
-            mm(chain(R(b, S_(0, 1)), *[(R("bo32"), R("asum", S_(i, i + 1))) for i in range(2 * t + 2)]))
-            cp(R("ai"), R(b, S_(0, 1)))
+            a = R("po", S_(0, 1))
+            mm(chain(a, *[(R("bo32"), R("asum", S_(i, i + 1))) for i in range(2 * t + 2)]))
+            cp(R("ai"), a)
             ts(R("a31"), R("ai"), 31, A.bitwise_and)
             ts(R("nlim", S_(t + 1, t + 2)), R("a31"), -8.0, A.mult, R("thn"), A.add)
         ts(R("KTf", h), R("T1", h), -2047.5, A.is_gt)
@@ -328,13 +322,13 @@ def program(nrem):
     def stageC(t, h):
         k, last = 2 * t + h, t == NV - 1
         SG, Ib = R("SG", h), R("Ib")
+        p0, p1 = R("r2", S_(0, 128)), R("r2", S_(128, 256))
         for x, held, cw, eq, c1, m, keep, one, snd, land, low in (("t", "Tq", "sw", "eqC", "C1t", "Tm", "KTf", "T1", "stt", "tt", -2050.0),
                                                                   ("d", "Dq", "cw", "eqB", "C1", "Dm", "KD", "D1", "sd", "dt", -2048.0)):
             member(cw, held, eq, h)
-            b = ring()
-            p0, p1 = R(b, S_(0, 128)), R(b, S_(128, 256))
+            cnt = counts(eq, "cm" + eq[2], h, "pk")
             mm(chain(p1, (R("I16"), R(one, h)), (R("Ib4096n"), SG), (Ib, R("cm4096"))) +
-               chain(p0, (Ib, R("c67584")), (R("Ib65536"), SG), (R("Im16"), R(keep, h)), *counts(eq, h)))
+               chain(p0, (Ib, R("c67584")), (R("Ib65536"), SG), (R("Im16"), R(keep, h)), cnt))
             tt(R(c1, h), R(cw, h), p0, A.min)
             tt(R(m, h), R(c1, h), p1, A.max)
             if last:
@@ -344,37 +338,32 @@ def program(nrem):
                 ts(R(snd, k), R(m, h), low, A.max, 2063.0, A.add)
                 send(t, h, x, snd, land)
         scan(R("xs", h), R("rst"), R("XG", h))
-        b = ring()
-        c = [R(b, blk(i)) for i in range(3)]
+        c = [R("pc", blk(i)) for i in range(4)]
         ys = R("ysb", h)
         mm(chain(c[0], (R("Ibh"), ys), (R("Ibh"), R("xs", h, S_(15, 2048, 16))), (R("Ib512n"), SG)) +
            chain(c[1], (Ib, R("zl", k)), (R("Ib256"), SG)) + chain(c[2], (Ib, ys), (R("Ib256n"), R("SA", h))))
         ts(R("hf", h), c[0], 511.75, A.add, 1024.0, A.max)
         act(R("zg", h), c[1], F.Relu, bias=R("cst", S_(2, 3)))
         act(R("yg", h), c[2], F.Relu, bias=R("cst", S_(2, 3)))
-        p = R(ring(), S_(0, 128))
-        mm(chain(p, (R("I16"), R("hf", h)), (Ib, R("zg", h)), (R("Ibn"), R("yg", h))))
-        act(R("oz", blk(h)) if last else R("sz", k), p, F.Abs, bias=R("cst", S_(3, 4)))
+        mm(chain(c[3], (R("I16"), R("hf", h)), (Ib, R("zg", h)), (R("Ibn"), R("yg", h))))
+        act(R("oz", blk(h)) if last else R("sz", k), c[3], F.Abs, bias=R("cst", S_(3, 4)))
         if last:
             out("yz", "oz", blk(h))
         else:
             send(t, h, "z", "sz", "zl")
 
     def stageD(t):
-        last = t == NV - 1
+        last, b = t == NV - 1, "po"
         for h in (0, 1):
             tt(R("dvq", blk(h, 8)), R("nv", h, S_(0, 8)), R("q0", blk(h, 8)), A.subtract)
         tt(R("mvq"), R("dvq"), R("pr"), A.mult)
         tt(R("PV16"), R("mvq"), R("q0"), A.add)
         tt(R("PV"), R("mvq"), R("q0"), A.add)
-        b = ring()
         mm([(R(b, S_(r, 256, 16)), R("I16"), R("PV16"), True, True) for r in range(16)])
         act(R("PVs"), R(b, S_(0, 256)), F.Copy)
-        b = ring()
         mm([(R(b, S_(0, 256)), R("I16"), R("tri"), True, False)] +
            [(R(b, S_(r, 256, 16)), R("bc", blk(r)), R("PV16"), False, r == 15) for r in range(16)])
         tt(R("eqP"), R("PVs"), R(b, S_(0, 256)), A.is_equal)
-        b = ring()
         mm(chain(R(b, S_(0, 16)), *[(R("selm", blk(r)), R("eqP", S_(r, 256, 16))) for r in range(16)]))
         tt(R("dq2"), R("q0"), R("PV"), A.subtract)
         ts(R("lm"), R(b, S_(0, 16)), -1.0, A.is_lt)
@@ -386,7 +375,7 @@ def program(nrem):
             ts(R("ysw", S_(0, 1024)), R("scw", S_(0, 1024)), 2047.0, A.add, -1.0, A.max)
         for c in range(16):
             o, off, src = R(win), R("PLu", S_(2 * c, 2 * c + 1)), R("T1s", blk(c, 16))
-            add("V", OVV + 64, lambda g, T, o=o, off=off, src=src: g.vector.tensor_copy(get(T, o).indirect(get(T, off)), get(T, src)), [off, src], [o])
+            add("V", 100, lambda g, T, o=o, off=off, src=src: g.vector.tensor_copy(get(T, o).indirect(get(T, off)), get(T, src)), [off, src], [o])
         if last:
             out("ys", "ysw", S_(0, 1024))
 

@@ -13,20 +13,21 @@ def _decl(text, d, lead):
 
 
 _decl("tli:256 dli:256 thi:1 sci:1024 sti:1024 pidx:1 pmi:1 ai:1 a31:1", i32, [])
-_decl("tm0:256 ts0:256 stm:1024 sta:1024 stw:1024 scw:1280 ysw:1280 pmf:1 iq:384 P1:16 on32:128 boa:128 bo32:128 id32:128 "
-      "q0i:16 q0:16 thn:1 nlim:8 asum:16 T1s:256 pr:16 dvq:16 mvq:16 PV:16 PVs:256 lm:16 dq2:16 lq:16 PLf:16 od:256 ot:256 oz:256 cst:4", f32, [])
+_decl("tm0:256 ts0:256 stm:1024 sta:1024 stw:1024 scw:1280 pmf:1 iq:384 P1:16 on32:128 boa:128 bo32:128 id32:128 "
+      "q0i:16 q0:16 thn:1 nlim:8 asum:16 T1s:256 pr:16 dvq:16 mvq:16 PV:16 PVs:256 lm:16 dq2:16 lq:16 PLf:16 od:256 ot:256 oz:256 cst:5", f32, [])
 _decl("selm:2048 bc:2048 dM:384 tri:256 PV16:16 eqP:256", f16, [])
-_decl("clkw:4112 rst:2048 rowc:128 k8big:128", b16, [])
+_decl("clkw:4112 rst:2048 rs:128 rowc:128 k8big:128", b16, [])
 _decl("PLu:32", u16, [])
 _decl("eqA:2048 eqB:2048 eqC:2048 Dq:512 Tq:512 D1:128 KD:128 CD:128 T1a:128 CT:128 FC:128 oh:128 KT:128 T1:128 KTf:128 LMs:384 "
       "cw:128 sw:128 hf:128 dst:128", f16, [2])
-_decl("Y:2048 GA:16,128 XG:2048 xs:2048 rl:128 OHn:128 SG:128 SA:128 ac:128 acr:128 cmA:128 cmB:128 cmC:128 ysb:128 zg:128 yg:128", b16, [2])
-_decl("sk:128 sk2:128 a1:8 b1:8 sel:8 dvu:8 ms:8 wf:8 C1:128 C1t:128 Dm:128 Tm:128", f32, [2])
+_decl("Y:2048 GA:16,128 XG:2048 xs:2048 rl:128 OHn:128 SG:128 SA:128 ac:128 acr:128 cmA:128 cmB:128 cmC:128 ysb:128 zg:128 yg:128 "
+      "sdB:512 sdC:512 seB:512 seC:512", b16, [2])
+_decl("sk:128 sk2:128 a1:8 dvu:8 ms:8 wf:8 C1:128 C1t:128 Dm:128 Tm:128", f32, [2])
 _decl("nu:16 nv:16", i32, [2])
 _decl("D1u:128 nlu:8 wu:8", u16, [2])
 _decl("dt:128 tt:128 sd:128 stt:128", u16, [2 * NV])
 _decl("zl:128 sz:128", b16, [2 * NV])
-for _b, _l, _d in (("kh", "I16 Im16 BOm16 BO16 BOm128 c2048 c2040 c16320n I8n o128h cm2047", f16),
+for _b, _l, _d in (("kh", "I16 In16 Im16 BOm16 BO16 BO128 BOm128 c2048 c2040 c16320n I8n o128h cm2047", f16),
                    ("kb", "Ib Ibn Ibh Ib512n Ib256 Ib256n Ib4096n Ib65536 I4128n BO64b BOb c67584 cm4096 o128b", b16)):
     _l = _l.split()
     SCRATCH[_b] = ("sbuf", [128, len(_l), 128], _d)
@@ -35,10 +36,12 @@ for _b, _l, _d in (("kh", "I16 Im16 BOm16 BO16 BOm128 c2048 c2040 c16320n I8n o1
 for _n in ("pc", "po", "pk", "r0", "r1", "r2"):
     SCRATCH[_n] = ("psum", [128, 512], f32)
 SCRATCH["pg0"] = SCRATCH["pg1"] = ("psum", [128, 8, 64], f32)
+BK = dict(cnt="po", dist="pk", ca="po", key="r2", oh="r2", lm="pc", ll="r2", tot="pc", h="r2", cc="r2", z="pc", d="po", d2="pk")
 LOADS = ("tl", "dl", "za", "zb", "th", "clk", "st", "sc")
 SEMAPHORES = ["sv", "ss", "sp", "sg", "so", "ls"] + ["l_" + n for n in LOADS]
 SEMAPHORES += ["a%d%d%s" % (t, h, k) for t in range(1, NV) for h in (0, 1) for k in "dtz"]
-CYC, OVV, OVS, WAKE, SELF, REMOTE = 0.9, 10.0, 20.0, 70.0, 50.0, 3000.0
+CYC, OVV, OVS, WAKE, SELF, REMOTE, LOOK = 1.0, 10.0, 20.0, 70.0, 100.0, 4000.0, 20.0
+BIAS = {"D": -5.0, "B0": 20.0, "B1": 60.0, "A1": -5.0, "C1": -5.0}
 
 
 def R(name, *ix):
@@ -85,10 +88,10 @@ def two(*xs):
 
 
 def program(nrem):
-    ops, rc = [], [0]
+    ops, rc, lab = [], [0], [""]
 
     def add(e, dur, fn, r, w, **kw):
-        ops.append(dict(kw, e=e, d=dur, fn=fn, r=[x for x in r if isinstance(x, tuple)], w=w))
+        ops.append(dict(kw, g=lab[0], e=e, d=dur, fn=fn, r=[x for x in r if isinstance(x, tuple)], w=w))
         return len(ops) - 1
 
     def val(T, x):
@@ -123,7 +126,9 @@ def program(nrem):
     def gat(e, o, win, off):
         def fn(g, T):
             x = get(T, win).indirect(get(T, off))
-            return g.vector.tensor_copy(get(T, o), x) if e == "V" else g.scalar.activation(get(T, o), x, F.Copy)
+            if e == "S":
+                return g.scalar.activation(get(T, o), x, F.Copy)
+            return g.vector.tensor_copy(get(T, o), x) if win[0] == "stw" else g.vector.tensor_scalar(get(T, o), x, -2047.0, None, A.add)
         add(e, 75 + 1.5 * size(o) * CYC, fn, [win, off], [o])
 
     def mm(lst):
@@ -153,8 +158,8 @@ def program(nrem):
         kw = {} if SCRATCH[o[0]][2] == i32 else {"allow_small_or_imprecise_dtypes": True}
         add("G", 130 + 2 * size(o), lambda g, T: g.iota(get(T, o), pat, base, cm, **kw), [], [o])
 
-    def aff(o, i, pat, op, base, cm):
-        add("G", 170 + 2 * size(o), lambda g, T: g.affine_select(get(T, o), get(T, i), pat, op, 0.0, base, cm), [i], [o])
+    def aff(o, i, pat, op, base, cm, other=0.0):
+        add("G", 170 + 2 * size(o), lambda g, T: g.affine_select(get(T, o), get(T, i), pat, op, other, base, cm), [i], [o])
     fill(R("on32"), 1.0)
     iota(R("pidx"), [[0, 1]], 0, 1)
     aff(R("boa"), R("on32"), [[-16, 8], [0, 16]], A.is_ge, 0, 1)
@@ -170,7 +175,8 @@ def program(nrem):
     for j in range(16):
         ts(R("bc", blk(j)), R("bo32"), R("P1", S_(j, j + 1)), A.mult)
     fill(R("clkw", S_(0, 16)), -1.0)
-    for n, src, k in (("I16", "id32", 1), ("Im16", "id32", -4112), ("BO16", "bo32", 1), ("BOm16", "bo32", -4112), ("BOm128", "bo32", -128),
+    for n, src, k in (("I16", "id32", 1), ("In16", "id32", -1), ("Im16", "id32", -4112), ("BO16", "bo32", 1), ("BOm16", "bo32", -4112),
+                      ("BOm128", "bo32", -128), ("BO128", "bo32", 128),
                       ("Ib", "id32", 1), ("Ibn", "id32", -1), ("I4128n", "id32", -4128), ("BOb", "bo32", 1), ("BO64b", "bo32", 64),
                       ("Ibh", "id32", 0.5), ("Ib512n", "id32", -512), ("Ib256", "id32", 256), ("I8n", "id32", -8), ("k8big", "bo32", 8),
                       ("Ib256n", "id32", -256), ("Ib4096n", "id32", -4096), ("Ib65536", "id32", 65536)):
@@ -180,11 +186,13 @@ def program(nrem):
             ts(R(n), R(src), float(k), A.mult)
     for j in range(16):
         aff(R("selm", blk(j)), R("BOm16"), [[0, 8], [1, 16]], A.is_equal, -j, 0)
+    iota(R("rst"), [[0, 128], [1, 16]], 0)
+    aff(R("rst"), R("rst"), [[0, 128], [1, 16]], A.is_equal, 0, 0, 1.0)
     for n, x in (("c2048", 2048.0), ("o128b", 1.0 / 128), ("o128h", 1.0 / 128), ("cm2047", -2047.0), ("c2040", 2040.0), ("c16320n", -16320.0),
-                 ("c67584", 67584.0), ("cm4096", -4096.0), ("rst", 1.0)):
+                 ("c67584", 67584.0), ("cm4096", -4096.0), ("rs", 1.0)):
         fill(R(n), x)
-    fill(R("rst", S_(0, 2048, 16)), 0.0)
-    for i, x in enumerate((64.5, 0.5, -256.0, -1024.0)):
+    fill(R("rs", S_(0, 128, 16)), 0.0)
+    for i, x in enumerate((64.5, 0.5, -256.0, -1024.0, 1.0)):
         fill(R("cst", S_(i, i + 1)), x)
     ts(R("dM"), R("iq"), pm, A.is_equal)
     ts(R("tri"), R("iq", S_(0, 256)), pm, A.is_ge, 5000.0, A.mult)
@@ -201,7 +209,7 @@ def program(nrem):
         ts(R("stm", c), R("sti", c), 0.0, A.min, 2.0, A.mult)
         tt(R("sta", c), R("sti", c), R("stm", c), A.add)
         act(R("stw", c), R("sta", c), F.Copy, bias=-2047.0)
-    ts(R("scw", S_(0, 1024)), R("sci"), -2047.0, A.add)
+    cp(R("scw", S_(0, 1024)), R("sci"))
 
     WIN = R("clkw")
     sent = {}
@@ -219,11 +227,18 @@ def program(nrem):
         for q in range(4):
             rc[0] += 1
             b = "r%d" % (rc[0] % 2)
-            mm([(R(b, blk(i)), R("bc", blk(4 * q + i)), R(rows, h, S_(0, 128)), True, True) for i in range(4)])
-            tt(R(eq, h, blk(q, 512)), R(held, h, S_(0, 512)), R(b, S_(0, 512)), A.is_equal)
+            if q == 0 and eq != "eqA":
+                mm(sum([chain(R(b, blk(i)), (R("bc", blk(i)), R(rows, h, S_(0, 128))), (R("In16"), R(held, h, S_(0, 128)))) for i in range(4)], []))
+                act(R("sd" + eq[2], h), R(b, S_(0, 512)), F.Abs)
+                act(R("se" + eq[2], h), R("sd" + eq[2], h), F.Relu, bias=R("cst", S_(4, 5)), scale=-1.0)
+            else:
+                mm([(R(b, blk(i)), R("bc", blk(4 * q + i)), R(rows, h, S_(0, 128)), True, True) for i in range(4)])
+                tt(R(eq, h, blk(q, 512)), R(held, h, S_(0, 512)), R(b, S_(0, 512)), A.is_equal)
 
     def counts(eq, cm, h, b):
-        mm([(R(b, S_(384 + j, 512, 16)), R(eq, h, blk(j)), R("BO16", S_(0, 128, 16)), True, True) for j in range(16)])
+        def one(j):
+            return (R("se" + eq[2], h, blk(j)), R("BOb", S_(0, 128, 16))) if j < 4 and eq != "eqA" else (R(eq, h, blk(j)), R("BO16", S_(0, 128, 16)))
+        mm([(R(b, S_(384 + j, 512, 16)),) + one(j) + (True, True) for j in range(16)])
         act(R(cm, h), R(b, S_(384, 512)), F.Copy)
         return (R(cm, h), R("I4128n"))
 
@@ -239,9 +254,9 @@ def program(nrem):
                 ts(R(dst, h, blk(r)), R(src, k), -2063.0, A.add)
         D, Tn = R("Dq", h, S_(0, 128)), R("Tq", h, S_(0, 128))
         member("Tq", "Dq", "eqA", h)
-        pD, pT, c = R("pc", S_(0, 128)), R("pc", S_(128, 256)), (R("I16"), R("c2048"))
+        pD, pT, c = R(BK["cnt"], S_(0, 128)), R(BK["cnt"], S_(128, 256)), (R("I16"), R("c2048"))
         mm(chain(pD, c, *[(R("Im16"), R("eqA", h, blk(j))) for j in range(16)]))
-        mm(chain(pT, c, counts("eqA", "cmA", h, "po")))
+        mm(chain(pT, c, counts("eqA", "cmA", h, BK["ca"])))
         tt(R("D1", h), D, pD, A.min)
         tt(R("T1a", h), Tn, pT, A.min)
         ts(R("D1u", h), R("D1", h), -2048.0, A.max, 2063.0, A.add)
@@ -254,8 +269,8 @@ def program(nrem):
                 mm(sum([chain(R(b, i), (R("Ib"), R("Y", h, S_(1024 * hb + 8 * q + i, 1024 * hb + 1024, 16))), (R("Ibn"), R("zl", k, blk(hb, 64))))
                         for i in range(8)], []))
                 act(R("GA", h, blk(q, 8), blk(hb, 64)), R(b), F.Abs)
-        d = R("pc", S_(256, 384))
-        mm([(R("pc", S_(256 + j, 384, 16)), R("GA", h, j), R("BOb", S_(0, 128, 16)), True, True) for j in range(16)])
+        d = R(BK["dist"], S_(256, 384))
+        mm([(R(BK["dist"], S_(256 + j, 384, 16)), R("GA", h, j), R("BOb", S_(0, 128, 16)), True, True) for j in range(16)])
         ts(R("dst", h), d, -2040.0, A.add)
         mm(chain(d, (R("dst", h), R("I16")), (R("I16"), R("c2040"))))
         act(R("rl", h), d, F.Relu, bias=R("nlim", S_(t, t + 1)))
@@ -263,41 +278,40 @@ def program(nrem):
     def stageB(t, h):
         k = 2 * t + h
         Z, Tn = R("zl", k), R("Tq", h, S_(0, 128))
-        kk, rs = R("pk", S_(0, 128)), R("rst", S_(0, 128))
+        kk, rs = R(BK["key"], S_(0, 128)), R("rs")
         mm([(kk, Z, R("k8big"), True, False), (kk, R("o128b"), R("rowc"), False, False), (kk, R("o128h"), R("c16320n"), False, False)] +
-           [(R("pk", S_(j, 128, 16)), R("Y", h, S_(j, 2048, 16)), R("k8big", S_(0, 128, 16)), False, False) for j in range(16)] +
+           [(R(BK["key"], S_(j, 128, 16)), R("Y", h, S_(j, 2048, 16)), R("k8big", S_(0, 128, 16)), False, False) for j in range(16)] +
            [(kk, R("I8n"), R("dst", h), False, True)])
         scan(R("sk", h), rs, kk)
         cp(R("sk", h, S_(0, 128, 16)), R("sk", h, S_(15, 128, 16)))
         scan(R("sk2", h), rs, R("sk", h))
         tt(R("oh", h), R("sk2", h), kk, A.is_equal)
-        o1, o2 = R("po", S_(0, 128)), R("po", S_(128, 256))
+        o1, o2 = R(BK["oh"], S_(0, 128)), R(BK["oh"], S_(128, 256))
         mm(chain(o1, (R("oh", h), R("I16"))) + chain(o2, (R("oh", h), R("Im16")), (R("I16"), R("c2048"))))
         tt(R("KT", h), Tn, o1, A.mult)
         act(R("OHn", h), o1, F.Copy)
         tt(R("FC", h), R("rl", h), R("CT", h), A.min)
         tt(R("T1", h), R("T1a", h), o2, A.min)
-        b = "r2"
+        b = BK["lm"]
         c = [R(b, blk(i)) for i in range(4)]
         KD, FC, OHn, KT, BO = R("KD", h), R("FC", h), R("OHn", h), R("KT", h), R("BO16")
         mm(chain(c[2], (R("o128h"), R("cm2047")), (Z, R("BOb"))) + chain(c[1], (KT, BO)) +
-           chain(c[0], (KD, BO), (FC, R("BOm128")), (OHn, R("BO64b"))) + chain(c[3], (BO, KD), (R("BOm128"), FC), (R("BO64b"), OHn)))
+           chain(c[0], (KD, BO), (FC, R("BO128")), (OHn, R("BO64b"))) + chain(c[3], (BO, KD), (R("BOm128"), FC), (R("BO64b"), OHn)))
         tt(R("LMs", h), R("dM"), R(b, S_(0, 384)), A.mult)
         tt(R("ac", h), R("CD", h), c[3], A.min)
         act(R("SG", h), c[3], F.Sign, bias=R("cst", S_(0, 1)), scale=-1.0)
         act(R("SA", h), c[3], F.Sign, bias=R("cst", S_(1, 2)))
+        b = BK["ll"]
         mm([(R(b, blk(i, 8)), R("LMs", h, blk(i)), R("BO16", S_(0, 128, 16)), True, True) for i in range(3)])
         X, E = R(b, S_(0, 8)), R(b, S_(8, 16))
         ts(R("nu", h), R(b, S_(8, 24)), 2047.0, A.add)
         ts(R("a1", h), X, 64.5, A.is_gt)
-        ts(R("b1", h), X, -0.5, A.is_lt)
         ts(R("nv", h), R("nu", h), 1023, A.bitwise_and)
         ts(R("nlu", h), E, 2063.0, A.add)
-        tt(R("sel", h), R("a1", h), R("b1", h), A.add)
         v, u = R("nv", h, S_(0, 8)), R("nv", h, S_(8, 16))
         tt(R("dvu", h), v, u, A.subtract)
         ts(R("pr", blk(h, 8)), X, 64.0, A.is_equal)
-        tt(R("ms", h), R("dvu", h), R("sel", h), A.mult)
+        tt(R("ms", h), R("dvu", h), R("a1", h), A.mult)
         tt(R("wf", h), R("ms", h), u, A.add)
         cp(R("wu", h), R("wf", h))
         gat("V", R("sw", h), R("stw"), R("wu", h))
@@ -305,28 +319,27 @@ def program(nrem):
         gat("S", R("ysb", h), WIN, R("nlu", h))
         act(R("acr", h), R("ac", h), F.Relu, acc=R("asum", S_(k, k + 1)))
         if t + 1 < NV and h == 1:
-            a = R("po", S_(0, 1))
+            a = R(BK["tot"], S_(0, 1))
             mm(chain(a, *[(R("bo32"), R("asum", S_(i, i + 1))) for i in range(2 * t + 2)]))
             cp(R("ai"), a)
             ts(R("a31"), R("ai"), 31, A.bitwise_and)
             ts(R("nlim", S_(t + 1, t + 2)), R("a31"), -8.0, A.mult, R("thn"), A.add)
         ts(R("KTf", h), R("T1", h), -2047.5, A.is_gt)
-        last = t == NV - 1
-        ts(R("T1s", blk(h)), R("T1", h), 2047.0 if last else 0.0, A.add, -1.0 if last else -2048.0, A.max)
+        ts(R("T1s", blk(h)), R("T1", h), 2047.0, A.add, -1.0, A.max)
         for hb in (0, 1):
             gat("S", R("XG", h, blk(hb, 1024)), WIN, R("D1u", h, blk(hb, 64)))
 
-    def out(name, buf, c):
-        add("Y", 60, lambda g, T: g.sync.dma_start(T[name][:, c], get(T, R(buf, c))), [R(buf, c)], [], tok="so")
+    def out(name, buf, c, lat=2500):
+        add("Y", 60, lambda g, T: g.sync.dma_start(T[name][:, c], get(T, R(buf, c))), [R(buf, c)], [], tok="so", lat=lat)
 
     def stageC(t, h):
         k, last = 2 * t + h, t == NV - 1
         SG, Ib = R("SG", h), R("Ib")
-        p0, p1 = R("r2", S_(0, 128)), R("r2", S_(128, 256))
+        p0, p1 = R(BK["h"], S_(0, 128)), R(BK["h"], S_(128, 256))
         for x, held, cw, eq, c1, m, keep, one, snd, land, low in (("t", "Tq", "sw", "eqC", "C1t", "Tm", "KTf", "T1", "stt", "tt", -2050.0),
                                                                   ("d", "Dq", "cw", "eqB", "C1", "Dm", "KD", "D1", "sd", "dt", -2048.0)):
             member(cw, held, eq, h)
-            cnt = counts(eq, "cm" + eq[2], h, "pk")
+            cnt = counts(eq, "cm" + eq[2], h, BK["cc"])
             mm(chain(p1, (R("I16"), R(one, h)), (R("Ib4096n"), SG), (Ib, R("cm4096"))) +
                chain(p0, (Ib, R("c67584")), (R("Ib65536"), SG), (R("Im16"), R(keep, h)), cnt))
             tt(R(c1, h), R(cw, h), p0, A.min)
@@ -338,7 +351,7 @@ def program(nrem):
                 ts(R(snd, k), R(m, h), low, A.max, 2063.0, A.add)
                 send(t, h, x, snd, land)
         scan(R("xs", h), R("rst"), R("XG", h))
-        c = [R("pc", blk(i)) for i in range(4)]
+        c = [R(BK["z"], blk(i)) for i in range(4)]
         ys = R("ysb", h)
         mm(chain(c[0], (R("Ibh"), ys), (R("Ibh"), R("xs", h, S_(15, 2048, 16))), (R("Ib512n"), SG)) +
            chain(c[1], (Ib, R("zl", k)), (R("Ib256"), SG)) + chain(c[2], (Ib, ys), (R("Ib256n"), R("SA", h))))
@@ -353,14 +366,14 @@ def program(nrem):
             send(t, h, "z", "sz", "zl")
 
     def stageD(t):
-        last, b = t == NV - 1, "po"
+        b, b2 = BK["d"], BK["d2"]
         for h in (0, 1):
             tt(R("dvq", blk(h, 8)), R("nv", h, S_(0, 8)), R("q0", blk(h, 8)), A.subtract)
         tt(R("mvq"), R("dvq"), R("pr"), A.mult)
         tt(R("PV16"), R("mvq"), R("q0"), A.add)
         tt(R("PV"), R("mvq"), R("q0"), A.add)
-        mm([(R(b, S_(r, 256, 16)), R("I16"), R("PV16"), True, True) for r in range(16)])
-        act(R("PVs"), R(b, S_(0, 256)), F.Copy)
+        mm([(R(b2, S_(r, 256, 16)), R("I16"), R("PV16"), True, True) for r in range(16)])
+        act(R("PVs"), R(b2, S_(0, 256)), F.Copy)
         mm([(R(b, S_(0, 256)), R("I16"), R("tri"), True, False)] +
            [(R(b, S_(r, 256, 16)), R("bc", blk(r)), R("PV16"), False, r == 15) for r in range(16)])
         tt(R("eqP"), R("PVs"), R(b, S_(0, 256)), A.is_equal)
@@ -370,19 +383,17 @@ def program(nrem):
         tt(R("lq"), R("lm"), R("dq2"), A.mult)
         tt(R("PLf"), R("lq"), R("PV"), A.add)
         cp(R("PLu", S_(0, 32, 2)), R("PLf"))
-        win = "ysw" if last else "scw"
-        if last:
-            ts(R("ysw", S_(0, 1024)), R("scw", S_(0, 1024)), 2047.0, A.add, -1.0, A.max)
         for c in range(16):
-            o, off, src = R(win), R("PLu", S_(2 * c, 2 * c + 1)), R("T1s", blk(c, 16))
+            o, off, src = R("scw"), R("PLu", S_(2 * c, 2 * c + 1)), R("T1s", blk(c, 16))
             add("V", 100, lambda g, T, o=o, off=off, src=src: g.vector.tensor_copy(get(T, o).indirect(get(T, off)), get(T, src)), [off, src], [o])
-        if last:
-            out("ys", "ysw", S_(0, 1024))
+        if t == NV - 1:
+            out("ys", "scw", S_(0, 1024), 4500)
 
     for t in range(NV):
-        for stage in (stageA, stageB, stageC):
-            stage(t, 0)
-            stage(t, 1)
+        for s, f, h in (("A0", stageA, 0), ("B0", stageB, 0), ("A1", stageA, 1), ("B1", stageB, 1), ("C0", stageC, 0), ("C1", stageC, 1)):
+            lab[0] = s
+            f(t, h)
+        lab[0] = "D"
         stageD(t)
     return ops
 
@@ -420,12 +431,12 @@ def schedule(ops):
     fin = [o["d"] + o.get("lat", 0.0) for o in ops]
     pri = [0.0] * n
     for i in range(n - 1, -1, -1):
-        pri[i] = fin[i] + max([0.0] + [l + pri[k] for k, l in succ[i]])
+        pri[i] = BIAS.get(ops[i]["g"], 0.0) + fin[i] + max([0.0] + [l + pri[k] for k, l in succ[i]])
     rdy, free, order = [0.0] * n, {}, []
     ready = [i for i in range(n) if cnt[i] == 0]
     while ready:
         st = {i: max(rdy[i], free.get(ops[i]["e"], 0.0)) for i in ready}
-        tmin = min(st.values()) + 1.0
+        tmin = min(st.values()) + LOOK
         i = max((j for j in ready if st[j] <= tmin), key=lambda j: pri[j])
         ready.remove(i)
         o, s = ops[i], st[i]

from concourse.mybir import AluOpType, ActivationFunctionType

A, F = AluOpType, ActivationFunctionType
NV = 5
f32, f16, b16, i32, u16 = "float32", "float16", "bfloat16", "int32", "uint16"
SCRATCH, ALIAS = {}, {}


def _decl(text, d, lead):
    for w in text.split():
        n, s = w.split(":")
        SCRATCH[n] = ("sbuf", [128] + lead + [int(x) for x in s.split(",")], d)


_decl("tli:256 dli:256 thi:1 sci:1024 sti:1024 pidx:1 pmi:1 ai:1 a31:1", i32, [])
_decl("tm0:256 ts0:256 stm:1024 sta:1024 stw:1024 scw:1280 pmf:1 iq:384 P1:16 on32:128 boa:128 bo32:128 id32:128 "
      "q0i:16 q0:16 thn:1 nlim:8 asum:16 T1s:256 pr:16 dvq:16 mvq:16 PV:16 PVs:256 lm:16 dq2:16 lq:16 PLf:16 od:256 ot:256 oz:256 cst:5", f32, [])
_decl("selm:2048 bc:2048 dM:384 tri:256 PV16:16 eqP:256", f16, [])
_decl("clkw:4112 rst:2048 rs:128 rowc:128 k8big:128", b16, [])
_decl("PLu:32", u16, [])
_decl("eqA:2048 eqB:2048 eqC:2048 Dq:512 Tq:512 D1:128 KD:128 CD:128 T1a:128 CT:128 FC:128 oh:128 KT:128 T1:128 KTf:128 LMs:384 "
      "cw:128 sw:128 hf:128 dst:128", f16, [2])
_decl("Y:2048 GA:16,128 XG:2048 xs:2048 rl:128 OHn:128 SG:128 SA:128 ac:128 acr:128 cmA:128 cmB:128 cmC:128 ysb:128 zg:128 yg:128 "
      "sdB:512 sdC:512 seB:512 seC:512", b16, [2])
_decl("sk:128 sk2:128 a1:8 dvu:8 ms:8 wf:8 C1:128 C1t:128 Dm:128 Tm:128", f32, [2])
_decl("nu:16 nv:16", i32, [2])
_decl("D1u:128 nlu:8 wu:8", u16, [2])
_decl("dt:128 tt:128 sd:128 stt:128", u16, [2 * NV])
_decl("zl:128 sz:128", b16, [2 * NV])
for _b, _l, _d in (("kh", "I16 In16 Im16 BOm16 BO16 BO128 BOm128 c2048 c2040 c16320n I8n o128h cm2047", f16),
                   ("kb", "Ib Ibn Ibh Ib512n Ib256 Ib256n Ib4096n Ib65536 I4128n BO64b BOb c67584 cm4096 o128b", b16)):
    _l = _l.split()
    SCRATCH[_b] = ("sbuf", [128, len(_l), 128], _d)
    for _i, _n in enumerate(_l):
        ALIAS[_n] = (_b, _i)
for _n in ("pc", "po", "pk", "r0", "r1", "r2"):
    SCRATCH[_n] = ("psum", [128, 512], f32)
SCRATCH["pg0"] = SCRATCH["pg1"] = ("psum", [128, 8, 64], f32)
BK = dict(cnt="po", dist="pk", ca="po", key="r2", oh="r2", lm="pc", ll="r2", tot="pc", h="r2", cc="r2", z="pc", d="po", d2="pk")
LOADS = ("tl", "dl", "za", "zb", "th", "clk", "st", "sc")
SEMAPHORES = ["sv", "ss", "sp", "sg", "so", "ls"] + ["l_" + n for n in LOADS]
SEMAPHORES += ["a%d%d%s" % (t, h, k) for t in range(1, NV) for h in (0, 1) for k in "dtz"]
CYC, OVV, OVS, WAKE, SELF, REMOTE, LOOK = 1.0, 10.0, 20.0, 70.0, 100.0, 4000.0, 20.0
BIAS = {"D": -5.0, "B0": 20.0, "B1": 60.0, "A1": -5.0, "C1": -5.0}


def R(name, *ix):
    return (ALIAS[name][0], (ALIAS[name][1],) + ix) if name in ALIAS else (name, ix)


def S_(a, b, st=None):
    return slice(a, b, st)


def blk(i, n=128):
    return slice(n * i, n * i + n)


def get(T, x):
    return T[x[0]][(slice(None),) + x[1] + (slice(None),) * (len(SCRATCH[x[0]][1]) - 1 - len(x[1]))]


def span(x):
    out = []
    for d, n in enumerate(SCRATCH[x[0]][1][1:]):
        i = x[1][d] if d < len(x[1]) else slice(None)
        if isinstance(i, int):
            out.append((i, i + 1, 1))
        else:
            a, b, st = i.indices(n)
            out.append((a, b, len(range(a, b, st))))
    return out


def size(x):
    n = 1
    for s in span(x):
        n *= s[2]
    return n


def psum(x):
    return SCRATCH[x[0]][0] == "psum"


def two(*xs):
    return all(not psum(x) and SCRATCH[x[0]][2] in (f16, b16, u16) for x in xs)


def program(nrem):
    ops, rc, lab = [], [0], [""]

    def add(e, dur, fn, r, w, **kw):
        ops.append(dict(kw, g=lab[0], e=e, d=dur, fn=fn, r=[x for x in r if isinstance(x, tuple)], w=w))
        return len(ops) - 1

    def val(T, x):
        return get(T, x) if isinstance(x, tuple) else x

    def ts(o, i, s1, op0, s2=None, op1=None):
        def fn(g, T):
            a = (get(T, o), get(T, i), val(T, s1), val(T, s2), op0)
            return g.vector.tensor_scalar(*(a if op1 is None else a + (op1,)))
        add("V", OVV + max(64, size(o) * (0.5 if two(o, i) else 1)) * CYC, fn, [i, s1, s2], [o])

    def tt(o, a, b, op):
        add("V", OVV + max(64, size(o) * (1 if psum(a) or psum(b) else 2)) * CYC,
            lambda g, T: g.vector.tensor_tensor(get(T, o), get(T, a), get(T, b), op), [a, b], [o])

    def cp(o, i):
        add("V", OVV + max(64, size(o)) * CYC, lambda g, T: g.vector.tensor_copy(get(T, o), get(T, i)), [i], [o])

    def fill(o, v):
        add("V", OVV + max(64, size(o)) * CYC, lambda g, T: g.vector.memset(get(T, o), v), [], [o])

    def scan(o, a, b):
        add("V", OVV + size(o) * (0.5 if two(o, a, b) else 1) * CYC,
            lambda g, T: g.vector.tensor_tensor_scan(get(T, o), get(T, a), get(T, b), 0.0, A.mult, A.max), [a, b], [o])

    def act(o, i, func, bias=0.0, scale=1.0, acc=None):
        def fn(g, T):
            kw = {} if acc is None else {"accum_out": get(T, acc)}
            return g.scalar.activation(get(T, o), get(T, i), func, bias=val(T, bias), scale=scale, **kw)
        add("S", OVS + max(64, size(o)) * CYC, fn, [i, bias], [o] + ([] if acc is None else [acc]))

    def gat(e, o, win, off):
        def fn(g, T):
            x = get(T, win).indirect(get(T, off))
            if e == "S":
                return g.scalar.activation(get(T, o), x, F.Copy)
            return g.vector.tensor_copy(get(T, o), x) if win[0] == "stw" else g.vector.tensor_scalar(get(T, o), x, -2047.0, None, A.add)
        add(e, 75 + 1.5 * size(o) * CYC, fn, [win, off], [o])

    def mm(lst):
        def fn(g, T):
            x = None
            for o, l, r, a, b in lst:
                x = g.tensor.matmul(get(T, o), get(T, l), get(T, r), a, b)
            return x
        d = sum(6 + max(64, size(m[0])) * 0.5 * (4 if SCRATCH[m[1][0]][2] == f32 else 1) for m in lst)
        add("P", 30 + d, fn, [m[1] for m in lst] + [m[2] for m in lst], [m[0] for m in lst])

    def chain(o, *pairs):
        return [(o, l, r, i == 0, i == len(pairs) - 1) for i, (l, r) in enumerate(pairs)]

    def load(q, name, o, src, dur):
        add(q, 60, lambda g, T: (g.sync if q == "Y" else g.scalar).dma_start(get(T, o), src(T)), [], [o], tok="l_" + name, lat=dur)
    load("S", "clk", R("clkw", S_(16, 4112)), lambda T: T.clk[:, :], 5000)
    load("Y", "tl", R("tli"), lambda T: T.tl[:, :], 2200)
    load("Y", "dl", R("dli"), lambda T: T.dl[:, :], 2500)
    load("Y", "za", R("zl", 0), lambda T: T.z0[:, 0:128], 2600)
    load("Y", "zb", R("zl", 1), lambda T: T.z0[:, 128:256], 2700)
    load("Y", "th", R("thi"), lambda T: T.th[:, :], 2800)
    load("Y", "st", R("sti"), lambda T: T.st[:, :], 6500)
    load("Y", "sc", R("sci"), lambda T: T.sc[:, :], 8000)

    def iota(o, pat, base, cm=0):
        kw = {} if SCRATCH[o[0]][2] == i32 else {"allow_small_or_imprecise_dtypes": True}
        add("G", 130 + 2 * size(o), lambda g, T: g.iota(get(T, o), pat, base, cm, **kw), [], [o])

    def aff(o, i, pat, op, base, cm, other=0.0):
        add("G", 170 + 2 * size(o), lambda g, T: g.affine_select(get(T, o), get(T, i), pat, op, other, base, cm), [i], [o])
    fill(R("on32"), 1.0)
    iota(R("pidx"), [[0, 1]], 0, 1)
    aff(R("boa"), R("on32"), [[-16, 8], [0, 16]], A.is_ge, 0, 1)
    aff(R("bo32"), R("boa"), [[16, 8], [0, 16]], A.is_ge, 15, -1)
    aff(R("id32"), R("on32"), [[-1, 128]], A.is_equal, 0, 1)
    iota(R("iq"), [[0, 24], [1, 16]], 0)
    iota(R("rowc"), [[0, 8], [-1, 16]], 16)
    iota(R("q0i"), [[16, 16]], 1024)
    ts(R("pmi"), R("pidx"), 15, A.bitwise_and)
    cp(R("pmf"), R("pmi"))
    pm = R("pmf", S_(0, 1))
    ts(R("P1"), R("iq", S_(0, 16)), pm, A.is_equal)
    for j in range(16):
        ts(R("bc", blk(j)), R("bo32"), R("P1", S_(j, j + 1)), A.mult)
    fill(R("clkw", S_(0, 16)), -1.0)
    for n, src, k in (("I16", "id32", 1), ("In16", "id32", -1), ("Im16", "id32", -4112), ("BO16", "bo32", 1), ("BOm16", "bo32", -4112),
                      ("BOm128", "bo32", -128), ("BO128", "bo32", 128),
                      ("Ib", "id32", 1), ("Ibn", "id32", -1), ("I4128n", "id32", -4128), ("BOb", "bo32", 1), ("BO64b", "bo32", 64),
                      ("Ibh", "id32", 0.5), ("Ib512n", "id32", -512), ("Ib256", "id32", 256), ("I8n", "id32", -8), ("k8big", "bo32", 8),
                      ("Ib256n", "id32", -256), ("Ib4096n", "id32", -4096), ("Ib65536", "id32", 65536)):
        if ALIAS.get(n, ("kb",))[0] == "kb":
            act(R(n), R(src), F.Copy, scale=float(k))
        else:
            ts(R(n), R(src), float(k), A.mult)
    for j in range(16):
        aff(R("selm", blk(j)), R("BOm16"), [[0, 8], [1, 16]], A.is_equal, -j, 0)
    iota(R("rst"), [[0, 128], [1, 16]], 0)
    aff(R("rst"), R("rst"), [[0, 128], [1, 16]], A.is_equal, 0, 0, 1.0)
    for n, x in (("c2048", 2048.0), ("o128b", 1.0 / 128), ("o128h", 1.0 / 128), ("cm2047", -2047.0), ("c2040", 2040.0), ("c16320n", -16320.0),
                 ("c67584", 67584.0), ("cm4096", -4096.0), ("rs", 1.0)):
        fill(R(n), x)
    fill(R("rs", S_(0, 128, 16)), 0.0)
    for i, x in enumerate((64.5, 0.5, -256.0, -1024.0, 1.0)):
        fill(R("cst", S_(i, i + 1)), x)
    ts(R("dM"), R("iq"), pm, A.is_equal)
    ts(R("tri"), R("iq", S_(0, 256)), pm, A.is_ge, 5000.0, A.mult)
    ts(R("q0"), R("q0i"), pm, A.add)
    ts(R("tm0"), R("tli"), 0.0, A.min, 2.0, A.mult)
    tt(R("ts0"), R("tli"), R("tm0"), A.add)
    for h in (0, 1):
        ts(R("tt", h), R("ts0", blk(h)), 16.0, A.add)
        ts(R("dt", h), R("dli", blk(h)), 16.0, A.add)
    ts(R("thn"), R("thi"), -1.0, A.mult)
    cp(R("nlim", S_(0, 1)), R("thn"))
    for k in range(2):
        c = blk(k, 512)
        ts(R("stm", c), R("sti", c), 0.0, A.min, 2.0, A.mult)
        tt(R("sta", c), R("sti", c), R("stm", c), A.add)
        act(R("stw", c), R("sta", c), F.Copy, bias=-2047.0)
    cp(R("scw", S_(0, 1024)), R("sci"))

    WIN = R("clkw")
    sent = {}

    def arrive(t, h, kind, buf):
        if t:
            add("R", 0, None, [], [R(buf, 2 * t + h)], tok="a%d%d%s" % (t, h, kind), inc=nrem, after=sent[(t - 1, h, kind)])

    def send(t, h, kind, src, buf):
        def fn(g, T):
            return get(T, R(buf, 2 * t + h + 2)), get(T, R(src, 2 * t + h)), "a%d%d%s" % (t + 1, h, kind)
        sent[(t, h, kind)] = add("G", 100, fn, [R(src, 2 * t + h)], [], n="send")

    def member(rows, held, eq, h):
        for q in range(4):
            rc[0] += 1
            b = "r%d" % (rc[0] % 2)
            if q == 0 and eq != "eqA":
                mm(sum([chain(R(b, blk(i)), (R("bc", blk(i)), R(rows, h, S_(0, 128))), (R("In16"), R(held, h, S_(0, 128)))) for i in range(4)], []))
                act(R("sd" + eq[2], h), R(b, S_(0, 512)), F.Abs)
                act(R("se" + eq[2], h), R("sd" + eq[2], h), F.Relu, bias=R("cst", S_(4, 5)), scale=-1.0)
            else:
                mm([(R(b, blk(i)), R("bc", blk(4 * q + i)), R(rows, h, S_(0, 128)), True, True) for i in range(4)])
                tt(R(eq, h, blk(q, 512)), R(held, h, S_(0, 512)), R(b, S_(0, 512)), A.is_equal)

    def counts(eq, cm, h, b):
        def one(j):
            return (R("se" + eq[2], h, blk(j)), R("BOb", S_(0, 128, 16))) if j < 4 and eq != "eqA" else (R(eq, h, blk(j)), R("BO16", S_(0, 128, 16)))
        mm([(R(b, S_(384 + j, 512, 16)),) + one(j) + (True, True) for j in range(16)])
        act(R(cm, h), R(b, S_(384, 512)), F.Copy)
        return (R(cm, h), R("I4128n"))

    def stageA(t, h):
        k = 2 * t + h
        arrive(t, h, "t", "tt")
        arrive(t, h, "d", "dt")
        arrive(t, h, "z", "zl")
        for hb in (0, 1):
            gat("S", R("Y", h, blk(hb, 1024)), WIN, R("tt", k, blk(hb, 64)))
        for dst, src in (("Tq", "tt"), ("Dq", "dt")):
            for r in range(4):
                ts(R(dst, h, blk(r)), R(src, k), -2063.0, A.add)
        D, Tn = R("Dq", h, S_(0, 128)), R("Tq", h, S_(0, 128))
        member("Tq", "Dq", "eqA", h)
        pD, pT, c = R(BK["cnt"], S_(0, 128)), R(BK["cnt"], S_(128, 256)), (R("I16"), R("c2048"))
        mm(chain(pD, c, *[(R("Im16"), R("eqA", h, blk(j))) for j in range(16)]))
        mm(chain(pT, c, counts("eqA", "cmA", h, BK["ca"])))
        tt(R("D1", h), D, pD, A.min)
        tt(R("T1a", h), Tn, pT, A.min)
        ts(R("D1u", h), R("D1", h), -2048.0, A.max, 2063.0, A.add)
        ts(R("CT", h), R("T1a", h), -2055.0, A.is_lt)
        ts(R("KD", h), R("D1", h), -2047.5, A.is_gt)
        ts(R("CD", h), R("D1", h), -2055.0, A.is_lt)
        for hb in (0, 1):
            for q in (0, 1):
                b = "pg%d" % q
                mm(sum([chain(R(b, i), (R("Ib"), R("Y", h, S_(1024 * hb + 8 * q + i, 1024 * hb + 1024, 16))), (R("Ibn"), R("zl", k, blk(hb, 64))))
                        for i in range(8)], []))
                act(R("GA", h, blk(q, 8), blk(hb, 64)), R(b), F.Abs)
        d = R(BK["dist"], S_(256, 384))
        mm([(R(BK["dist"], S_(256 + j, 384, 16)), R("GA", h, j), R("BOb", S_(0, 128, 16)), True, True) for j in range(16)])
        ts(R("dst", h), d, -2040.0, A.add)
        mm(chain(d, (R("dst", h), R("I16")), (R("I16"), R("c2040"))))
        act(R("rl", h), d, F.Relu, bias=R("nlim", S_(t, t + 1)))

    def stageB(t, h):
        k = 2 * t + h
        Z, Tn = R("zl", k), R("Tq", h, S_(0, 128))
        kk, rs = R(BK["key"], S_(0, 128)), R("rs")
        mm([(kk, Z, R("k8big"), True, False), (kk, R("o128b"), R("rowc"), False, False), (kk, R("o128h"), R("c16320n"), False, False)] +
           [(R(BK["key"], S_(j, 128, 16)), R("Y", h, S_(j, 2048, 16)), R("k8big", S_(0, 128, 16)), False, False) for j in range(16)] +
           [(kk, R("I8n"), R("dst", h), False, True)])
        scan(R("sk", h), rs, kk)
        cp(R("sk", h, S_(0, 128, 16)), R("sk", h, S_(15, 128, 16)))
        scan(R("sk2", h), rs, R("sk", h))
        tt(R("oh", h), R("sk2", h), kk, A.is_equal)
        o1, o2 = R(BK["oh"], S_(0, 128)), R(BK["oh"], S_(128, 256))
        mm(chain(o1, (R("oh", h), R("I16"))) + chain(o2, (R("oh", h), R("Im16")), (R("I16"), R("c2048"))))
        tt(R("KT", h), Tn, o1, A.mult)
        act(R("OHn", h), o1, F.Copy)
        tt(R("FC", h), R("rl", h), R("CT", h), A.min)
        tt(R("T1", h), R("T1a", h), o2, A.min)
        b = BK["lm"]
        c = [R(b, blk(i)) for i in range(4)]
        KD, FC, OHn, KT, BO = R("KD", h), R("FC", h), R("OHn", h), R("KT", h), R("BO16")
        mm(chain(c[2], (R("o128h"), R("cm2047")), (Z, R("BOb"))) + chain(c[1], (KT, BO)) +
           chain(c[0], (KD, BO), (FC, R("BO128")), (OHn, R("BO64b"))) + chain(c[3], (BO, KD), (R("BOm128"), FC), (R("BO64b"), OHn)))
        tt(R("LMs", h), R("dM"), R(b, S_(0, 384)), A.mult)
        tt(R("ac", h), R("CD", h), c[3], A.min)
        act(R("SG", h), c[3], F.Sign, bias=R("cst", S_(0, 1)), scale=-1.0)
        act(R("SA", h), c[3], F.Sign, bias=R("cst", S_(1, 2)))
        b = BK["ll"]
        mm([(R(b, blk(i, 8)), R("LMs", h, blk(i)), R("BO16", S_(0, 128, 16)), True, True) for i in range(3)])
        X, E = R(b, S_(0, 8)), R(b, S_(8, 16))
        ts(R("nu", h), R(b, S_(8, 24)), 2047.0, A.add)
        ts(R("a1", h), X, 64.5, A.is_gt)
        ts(R("nv", h), R("nu", h), 1023, A.bitwise_and)
        ts(R("nlu", h), E, 2063.0, A.add)
        v, u = R("nv", h, S_(0, 8)), R("nv", h, S_(8, 16))
        tt(R("dvu", h), v, u, A.subtract)
        ts(R("pr", blk(h, 8)), X, 64.0, A.is_equal)
        tt(R("ms", h), R("dvu", h), R("a1", h), A.mult)
        tt(R("wf", h), R("ms", h), u, A.add)
        cp(R("wu", h), R("wf", h))
        gat("V", R("sw", h), R("stw"), R("wu", h))
        gat("V", R("cw", h), R("scw", S_(0, 1024)), R("wu", h))
        gat("S", R("ysb", h), WIN, R("nlu", h))
        act(R("acr", h), R("ac", h), F.Relu, acc=R("asum", S_(k, k + 1)))
        if t + 1 < NV and h == 1:
            a = R(BK["tot"], S_(0, 1))
            mm(chain(a, *[(R("bo32"), R("asum", S_(i, i + 1))) for i in range(2 * t + 2)]))
            cp(R("ai"), a)
            ts(R("a31"), R("ai"), 31, A.bitwise_and)
            ts(R("nlim", S_(t + 1, t + 2)), R("a31"), -8.0, A.mult, R("thn"), A.add)
        ts(R("KTf", h), R("T1", h), -2047.5, A.is_gt)
        ts(R("T1s", blk(h)), R("T1", h), 2047.0, A.add, -1.0, A.max)
        for hb in (0, 1):
            gat("S", R("XG", h, blk(hb, 1024)), WIN, R("D1u", h, blk(hb, 64)))

    def out(name, buf, c, lat=2500):
        add("Y", 60, lambda g, T: g.sync.dma_start(T[name][:, c], get(T, R(buf, c))), [R(buf, c)], [], tok="so", lat=lat)

    def stageC(t, h):
        k, last = 2 * t + h, t == NV - 1
        SG, Ib = R("SG", h), R("Ib")
        p0, p1 = R(BK["h"], S_(0, 128)), R(BK["h"], S_(128, 256))
        for x, held, cw, eq, c1, m, keep, one, snd, land, low in (("t", "Tq", "sw", "eqC", "C1t", "Tm", "KTf", "T1", "stt", "tt", -2050.0),
                                                                  ("d", "Dq", "cw", "eqB", "C1", "Dm", "KD", "D1", "sd", "dt", -2048.0)):
            member(cw, held, eq, h)
            cnt = counts(eq, "cm" + eq[2], h, BK["cc"])
            mm(chain(p1, (R("I16"), R(one, h)), (R("Ib4096n"), SG), (Ib, R("cm4096"))) +
               chain(p0, (Ib, R("c67584")), (R("Ib65536"), SG), (R("Im16"), R(keep, h)), cnt))
            tt(R(c1, h), R(cw, h), p0, A.min)
            tt(R(m, h), R(c1, h), p1, A.max)
            if last:
                ts(R("o" + x, blk(h)), R(m, h), 2047.0, A.add, -1.0, A.max)
                out("y" + x, "o" + x, blk(h))
            else:
                ts(R(snd, k), R(m, h), low, A.max, 2063.0, A.add)
                send(t, h, x, snd, land)
        scan(R("xs", h), R("rst"), R("XG", h))
        c = [R(BK["z"], blk(i)) for i in range(4)]
        ys = R("ysb", h)
        mm(chain(c[0], (R("Ibh"), ys), (R("Ibh"), R("xs", h, S_(15, 2048, 16))), (R("Ib512n"), SG)) +
           chain(c[1], (Ib, R("zl", k)), (R("Ib256"), SG)) + chain(c[2], (Ib, ys), (R("Ib256n"), R("SA", h))))
        ts(R("hf", h), c[0], 511.75, A.add, 1024.0, A.max)
        act(R("zg", h), c[1], F.Relu, bias=R("cst", S_(2, 3)))
        act(R("yg", h), c[2], F.Relu, bias=R("cst", S_(2, 3)))
        mm(chain(c[3], (R("I16"), R("hf", h)), (Ib, R("zg", h)), (R("Ibn"), R("yg", h))))
        act(R("oz", blk(h)) if last else R("sz", k), c[3], F.Abs, bias=R("cst", S_(3, 4)))
        if last:
            out("yz", "oz", blk(h))
        else:
            send(t, h, "z", "sz", "zl")

    def stageD(t):
        b, b2 = BK["d"], BK["d2"]
        for h in (0, 1):
            tt(R("dvq", blk(h, 8)), R("nv", h, S_(0, 8)), R("q0", blk(h, 8)), A.subtract)
        tt(R("mvq"), R("dvq"), R("pr"), A.mult)
        tt(R("PV16"), R("mvq"), R("q0"), A.add)
        tt(R("PV"), R("mvq"), R("q0"), A.add)
        mm([(R(b2, S_(r, 256, 16)), R("I16"), R("PV16"), True, True) for r in range(16)])
        act(R("PVs"), R(b2, S_(0, 256)), F.Copy)
        mm([(R(b, S_(0, 256)), R("I16"), R("tri"), True, False)] +
           [(R(b, S_(r, 256, 16)), R("bc", blk(r)), R("PV16"), False, r == 15) for r in range(16)])
        tt(R("eqP"), R("PVs"), R(b, S_(0, 256)), A.is_equal)
        mm(chain(R(b, S_(0, 16)), *[(R("selm", blk(r)), R("eqP", S_(r, 256, 16))) for r in range(16)]))
        tt(R("dq2"), R("q0"), R("PV"), A.subtract)
        ts(R("lm"), R(b, S_(0, 16)), -1.0, A.is_lt)
        tt(R("lq"), R("lm"), R("dq2"), A.mult)
        tt(R("PLf"), R("lq"), R("PV"), A.add)
        cp(R("PLu", S_(0, 32, 2)), R("PLf"))
        for c in range(16):
            o, off, src = R("scw"), R("PLu", S_(2 * c, 2 * c + 1)), R("T1s", blk(c, 16))
            add("V", 100, lambda g, T, o=o, off=off, src=src: g.vector.tensor_copy(get(T, o).indirect(get(T, off)), get(T, src)), [off, src], [o])
        if t == NV - 1:
            out("ys", "scw", S_(0, 1024), 4500)

    for t in range(NV):
        for s, f, h in (("A0", stageA, 0), ("B0", stageB, 0), ("A1", stageA, 1), ("B1", stageB, 1), ("C0", stageC, 0), ("C1", stageC, 1)):
            lab[0] = s
            f(t, h)
        lab[0] = "D"
        stageD(t)
    return ops


def depend(ops):
    hist = {}
    for i, o in enumerate(ops):
        pw, acc = set(), {}
        for x, wr in [(x, False) for x in o["r"]] + [(x, True) for x in o["w"]]:
            sp = () if psum(x) else tuple(s[:2] for s in span(x))
            acc[(x[0], sp)] = acc.get((x[0], sp), False) or wr
        for (name, sp), wr in acc.items():
            for j, sj, wj in hist.get(name, ()):
                if j != i and all(a[0] < b[1] and b[0] < a[1] for a, b in zip(sp, sj)):
                    if wj or wr or ops[j]["e"] != o["e"] and SCRATCH[name][0] == "psum":
                        pw.add(j)
        for (name, sp), wr in acc.items():
            h = hist.setdefault(name, [])
            if wr:
                h[:] = [y for y in h if y[0] == i or not all(a[0] <= b[0] and b[1] <= a[1] for a, b in zip(sp, y[1]))]
            h.append((i, sp, wr))
        o["pw"] = pw


def schedule(ops):
    n = len(ops)
    succ, cnt = [[] for _ in range(n)], [0] * n
    for i, o in enumerate(ops):
        ps = [(j, WAKE if ops[j]["e"] != o["e"] else SELF) for j in o["pw"]]
        if "after" in o:
            ps.append((o["after"], REMOTE))
        cnt[i] = len(ps)
        for j, l in ps:
            succ[j].append((i, l))
    fin = [o["d"] + o.get("lat", 0.0) for o in ops]
    pri = [0.0] * n
    for i in range(n - 1, -1, -1):
        pri[i] = BIAS.get(ops[i]["g"], 0.0) + fin[i] + max([0.0] + [l + pri[k] for k, l in succ[i]])
    rdy, free, order = [0.0] * n, {}, []
    ready = [i for i in range(n) if cnt[i] == 0]
    while ready:
        st = {i: max(rdy[i], free.get(ops[i]["e"], 0.0)) for i in ready}
        tmin = min(st.values()) + LOOK
        i = max((j for j in ready if st[j] <= tmin), key=lambda j: pri[j])
        ready.remove(i)
        o, s = ops[i], st[i]
        o["s"] = s
        if o["e"] != "R":
            free[o["e"]] = s + o["d"]
        order.append(i)
        for k, l in succ[i]:
            cnt[k] -= 1
            rdy[k] = max(rdy[k], s + fin[i] + l)
            if cnt[k] == 0:
                ready.append(k)
    return order


CACHE = {}


def rank_program(g, core, T, topo):
    rank = T.rank_of(core)
    if rank is None:
        return
    dst = T.cores[(rank + 1) % len(T.cores)]
    rid, pid = topo.addr(dst)[:2]
    mask, nrem = topo.mask(core, dst), len(topo.engines(core, dst))
    if nrem not in CACHE:
        ops = program(nrem)
        depend(ops)
        CACHE[nrem] = (ops, schedule(ops))
    ops, order = CACHE[nrem]
    queue = {"V": g.vector, "S": g.scalar, "P": g.tensor, "G": g, "Y": g.sync}
    sem = {"V": "sv", "S": "ss", "P": "sp", "G": "sg"}
    known, vc, tok, total = {e: {} for e in queue}, {}, {}, {"ls": 0}
    for i in order:
        o = ops[i]
        e = o["e"]
        if e == "R":
            tok[i], vc[i] = (o["tok"], o["inc"]), {}
            total[o["tok"]] = o["inc"]
            continue
        kn, need = known[e], {}
        for j in o["pw"]:
            need[tok[j][0]] = max(need.get(tok[j][0], 0), tok[j][1])
        for j in sorted(o["pw"], reverse=True):
            s = tok[j][0]
            if kn.get(s, 0) < need[s]:
                queue[e].wait_ge(T.sem[s], need[s])
                kn[s] = need[s]
            for a in vc[j]:
                kn[a] = max(kn.get(a, 0), vc[j][a])
        x = o["fn"](g, T)
        if o.get("n") == "send":
            g.remote_dma(out_ap=x[0], in_ap=x[1], remote_sem=T.sem[x[2]], local_sem=T.sem["ls"], pid=pid, routing_id=rid, dma_engine_mask=mask)
            total["ls"] += nrem
            continue
        s, n = (o["tok"], 16) if "tok" in o else (sem[e], 1)
        total[s] = total.get(s, 0) + n
        x.then_inc(T.sem[s], n)
        tok[i], vc[i] = (s, total[s]), dict(kn)
    for s in total:
        if total[s]:
            g.wait_ge(T.sem[s], total[s])
